import numpy as np
import ml_dtypes


def mxq(x, axis, fmt="e4m3"):
    dtype, down = {"e4m3": (ml_dtypes.float8_e4m3fn, 7), "e5m2": (ml_dtypes.float8_e5m2, 14)}[fmt]
    v = np.moveaxis(np.asarray(x, np.float32).astype(ml_dtypes.bfloat16).astype(np.float64), axis, -1)
    blocks = v.reshape(v.shape[:-1] + (-1, 32))
    amax = np.abs(blocks).max(-1, keepdims=True)
    byte = np.maximum(np.where(amax > 0, np.frexp(amax)[1] - 1 + 127, 0) - down, 1)
    scale = np.exp2(byte - 127.0)
    codes = (blocks / scale).astype(np.float32).astype(dtype).astype(np.float64)
    return np.moveaxis((codes * scale).reshape(v.shape), -1, axis)


WIDE = False


def mx_kscale(k):
    if not WIDE:
        return np.ones(k)
    levels = np.array([10, -10, 5, -5, 0])
    if k % 512:
        return np.exp2(np.random.permutation(np.resize(levels, k // 32))).repeat(32)
    a = np.empty((k // 512, 16))
    for p in range(k // 512):
        a[p, :8] = np.random.permutation(np.resize(levels, 8))
        for g in range(8):
            far = levels[np.abs(levels - a[p, g]) >= 10]
            a[p, g + 8] = far[np.random.randint(len(far))]
    return np.exp2(a.ravel()).repeat(32)


def f64(x):
    return np.asarray(x).astype(np.float64)


def striped(idx):
    return np.tile(idx.reshape(-1, 16).T, (8, 1)).astype(np.uint16)


def unstriped(offs):
    return offs[:16].T.reshape(-1).astype(np.int64)


E2M1 = np.array([0.0, 0.5, 1.0, 1.5, 2.0, 3.0, 4.0, 6.0, -0.0, -0.5, -1.0, -1.5, -2.0, -3.0, -4.0, -6.0])


def pack_weight(w, fmt):
    k, n = w.shape
    w = f64(np.asarray(w, np.float32).astype(ml_dtypes.bfloat16)).reshape(k // 32, 32, n)
    amax = np.abs(w).max(1)
    if fmt == "e4m3":
        byte = np.frexp(amax)[1] - 1 + 127 - 7
    else:
        mant, ex = np.frexp(amax / 6.0)
        byte = np.where(mant > 0.5, ex, ex - 1) + 127
    byte = np.clip(np.where(amax > 0, byte, 1), 1, 254)
    scaled = (w * np.exp2(127.0 - byte)[:, None, :]).reshape(k, n).astype(np.float32)
    by_word = np.ascontiguousarray(scaled.reshape(k // 512, 128, 4, n).transpose(0, 1, 3, 2))
    if fmt == "e4m3":
        words = by_word.astype(ml_dtypes.float8_e4m3fn).view(np.uint8)
    else:
        c = by_word.astype(ml_dtypes.float4_e2m1fn).view(np.uint8) & 0xF
        words = (c[..., 0::2] | (c[..., 1::2] << 4)).reshape(k // 512, 128, 2 * n)
    return np.ascontiguousarray(words), np.ascontiguousarray(byte.astype(np.uint8).reshape(k // 512, 16, n))


def unpack_weight(words, scales, fmt):
    g, _, n = scales.shape
    words = np.ascontiguousarray(words).reshape(g, 128, n, -1)
    if fmt == "e4m3":
        vals = words.view(ml_dtypes.float8_e4m3fn).astype(np.float64)
    else:
        nib = np.empty((g, 128, n, 4), np.uint8)
        nib[..., 0::2] = words & 0xF
        nib[..., 1::2] = words >> 4
        vals = E2M1[nib]
    vals = vals * np.repeat(np.exp2(scales.astype(np.float64) - 127.0), 8, axis=1)[..., None]
    return vals.transpose(0, 1, 3, 2).reshape(g * 512, n)


def relu(v):
    return np.maximum(v, 0.0)


K, T, E, C, N = 1024, 2048, 6, 256, 128
K8 = 512


def by_expert(wq, xq):
    return np.concatenate([wq[e].T @ xq[:, e * C:(e + 1) * C] for e in range(E)], axis=1)


def setup_inputs():
    n = np.random.standard_normal
    s = mx_kscale(K)[:, None]
    w = n((E, K, N)) / np.sqrt(K) / s[None]
    w8 = [pack_weight(m[:K8], "e4m3") for m in w]
    w4 = [pack_weight(m[K8:], "e2m1") for m in w]
    return {
        "xT": (n((K, T)) * s).astype(np.float32),
        "w8_words": np.stack([m[0] for m in w8]),
        "w8_scales": np.stack([m[1] for m in w8]),
        "w4_words": np.stack([m[0] for m in w4]),
        "w4_scales": np.stack([m[1] for m in w4]),
        "b": (0.3 * n((N, E))).astype(np.float32),
        "gate": np.tile(np.random.uniform(0.2, 1.0, E * C), (N, 1)).astype(np.float32),
        "offs": striped(np.random.permutation(T)[:E * C]),
        "dst": striped(np.random.permutation(T)[:E * C]),
    }


def reference(xT, w8_words, w8_scales, w4_words, w4_scales, b, gate, offs, dst):
    idx = unstriped(offs)
    w = np.stack([np.concatenate([unpack_weight(w8_words[e], w8_scales[e], "e4m3"), unpack_weight(w4_words[e], w4_scales[e], "e2m1")]) for e in range(E)])
    xq = mxq(f64(xT)[:, idx], 0, "e4m3")
    y = by_expert(w, xq)
    y = relu(y + np.repeat(f64(b), C, axis=1))
    out = np.zeros((N, T))
    out[:, unstriped(dst)] = f64(gate) * y
    return out

@@ -1,0 +1,168 @@
+from contextlib import ExitStack
+
+import concourse.mybir as mybir
+
+K, T, E, C, N = 1024, 2048, 6, 256, 128
+S = E * C
+
+F32 = mybir.dt.float32
+BF16 = mybir.dt.bfloat16
+I32 = mybir.dt.int32
+U32 = mybir.dt.uint32
+U16 = mybir.dt.uint16
+U8 = mybir.dt.uint8
+E4M3X4 = mybir.dt.float8_e4m3fn_x4
+E2M1X4 = mybir.dt.float4_e2m1fn_x4
+COPY = mybir.ActivationFunctionType.Copy
+RELU = mybir.ActivationFunctionType.Relu
+MULT = mybir.AluOpType.mult
+
+FLOPS = 2 * K * N * S
+
+P = 128
+PACK = 4
+K_PASS = P * PACK
+PIECE = 512
+LOADS = (
+    (0, 0, 1024),
+    (0, 1024, 512),
+    (0, 1536, 512),
+    (1, 0, 1024),
+    (1, 1024, 768),
+    (1, 1792, 256),
+)
+PLANE_ROW = (4, 0)
+
+
+def tile_moe_two_lin_relu_kernel(
+    tc, xT, w8_words, w8_scales, w4_words, w4_scales, b, gate, offs, dst, out
+):
+    nc = tc.nc
+    with ExitStack() as ctx:
+        keep = ctx.enter_context(tc.tile_pool(name="keep", bufs=1))
+        stage = ctx.enter_context(tc.tile_pool(name="stage", bufs=len(LOADS)))
+        work = ctx.enter_context(tc.tile_pool(name="work", bufs=E))
+        psum = ctx.enter_context(tc.psum_pool(name="psum", bufs=E))
+
+        offs_sb = keep.tile([P, S // 16], U16, name="offs_sb")
+        dst_sb = keep.tile([P, S // 16], U16, name="dst_sb")
+        words = [keep.tile([P, T], U32, name=f"words{a}", align_bytes=64) for a in range(2)]
+        planes = keep.tile([P, T], U8, name="planes", align_bytes=64)
+        words_g = [keep.tile([P, S], U32, name=f"words_g{a}", align_bytes=64) for a in range(2)]
+        planes_g = keep.tile([P, S], U8, name="planes_g", align_bytes=64)
+        grouped = [keep.tile([P, T, PACK], BF16, name=f"grouped{a}", align_bytes=64) for a in range(2)]
+        w8_sb = keep.tile([P, E, 4 * N], U8, name="w8_sb", align_bytes=64)
+        w4_sb = keep.tile([P, E, 2 * N], U8, name="w4_sb", align_bytes=64)
+        w_planes = keep.tile([P, E, N], U8, name="w_planes", align_bytes=64)
+        bias = keep.tile([P, E], F32, name="bias")
+        gate_sb = keep.tile([P, S], F32, name="gate_sb")
+        out_sb = keep.tile([P, T], F32, name="out_sb")
+
+        nc.gpsimd.memset(w_planes[:].bitcast(I32), 0)
+        nc.gpsimd.memset(planes[:].bitcast(I32), 0)
+        nc.vector.memset(out_sb[:], 0.0)
+        for q in range(4):
+            nc.gpsimd.dma_start(
+                out=w_planes[32 * q + 4 : 32 * q + 8].bitcast(I32),
+                in_=w8_scales[:, :, 4 * q : 4 * q + 4, :].rearrange("e a q n -> q (e a) n").bitcast(I32),
+            )
+            nc.gpsimd.dma_start(
+                out=w_planes[32 * q : 32 * q + 4].bitcast(I32),
+                in_=w4_scales[:, :, 4 * q : 4 * q + 4, :].rearrange("e a q n -> q (e a) n").bitcast(I32),
+            )
+
+        raws = []
+        for i, (a, c0, width) in enumerate(LOADS):
+            raw = keep.tile([P, PACK, width], F32, name=f"raw{i}")
+            rows = xT[a * K_PASS : (a + 1) * K_PASS, c0 : c0 + width]
+            nc.sync.dma_start(out=raw[:], in_=rows.rearrange("(p j) w -> p j w", j=PACK))
+            raws.append(raw)
+            if i == 0:
+                nc.sync.dma_start(offs_sb[:], offs)
+        nc.sync.dma_start(out=w8_sb[:].bitcast(I32), in_=w8_words.rearrange("e a p n r -> p (e a) (n r)").bitcast(I32))
+        nc.sync.dma_start(out=w4_sb[:].bitcast(I32), in_=w4_words.rearrange("e a p n -> p (e a) n").bitcast(I32))
+        nc.sync.dma_start(out=bias[:], in_=b)
+        nc.sync.dma_start(dst_sb[:], dst)
+        nc.sync.dma_start(out=gate_sb[:], in_=gate)
+        acts = keep.tile([P, S], F32, name="acts")
+
+        def interleave(i, lo, hi, cut):
+            a, c0, width = LOADS[i]
+            for first, last, on_scalar in ((lo, cut, True), (cut, hi, False)):
+                if first == last:
+                    continue
+                to = grouped[a][:, c0 + first : c0 + last, :].rearrange("p (c i) j -> p c j i", i=4)
+                source = raws[i][:, :, first:last].rearrange("p j (c i) -> p c j i", i=4)
+                if on_scalar:
+                    nc.scalar.activation(to, source, COPY)
+                else:
+                    nc.vector.tensor_copy(out=to, in_=source)
+
+        def quantize(a, lo, hi):
+            nc.vector.quantize_mx(
+                out=words[a][:, lo:hi].bitcast(E4M3X4),
+                scales=planes[PLANE_ROW[a] : P, lo:hi],
+                in_=grouped[a][:, lo:hi, :].rearrange("p c j -> p (c j)"),
+            )
+
+        def gather(target, source, lo, hi):
+            nc.vector.tensor_copy(target[:, lo:hi], source[:].indirect(offs_sb[:, lo // 16 : hi // 16]))
+
+        def expert(e):
+            acc = psum.tile([P, C], F32, name="acc")
+            for h in range(0, C, 128):
+                cols = slice(e * C + h, e * C + h + 128)
+                nc.tensor.matmul_mx(
+                    out=acc[:, h : h + 128],
+                    lhsT=w8_sb[:, e, :].bitcast(E4M3X4),
+                    lhsT_scale=w_planes[PLANE_ROW[0] : P, e, :],
+                    rhs=words_g[0][:, cols].bitcast(E4M3X4),
+                    rhs_scale=planes_g[PLANE_ROW[0] : P, cols],
+                    start=True,
+                    stop=False,
+                )
+                nc.tensor.matmul_mx(
+                    out=acc[:, h : h + 128],
+                    lhsT=w4_sb[:, e, :].bitcast(E2M1X4),
+                    lhsT_scale=w_planes[PLANE_ROW[1] : P, e, :],
+                    rhs=words_g[1][:, cols].bitcast(E4M3X4),
+                    rhs_scale=planes_g[PLANE_ROW[1] : P, cols],
+                    start=False,
+                    stop=True,
+                )
+            nc.scalar.activation(acts[:, e * C : (e + 1) * C], acc[:], RELU, bias=bias[:, e : e + 1])
+
+        def scatter(lo, hi):
+            nc.vector.tensor_tensor(
+                out_sb[:].indirect(dst_sb[:, lo // 16 : hi // 16]), acts[:, lo:hi], gate_sb[:, lo:hi], MULT
+            )
+
+        interleave(0, 0, 512, 256)
+        interleave(0, 512, 1024, 768)
+        quantize(0, 0, 512)
+        quantize(0, 512, 1024)
+        interleave(1, 0, 512, 256)
+        quantize(0, 1024, 1536)
+        interleave(2, 0, 256, 96)
+        interleave(2, 256, 512, 352)
+        quantize(0, 1536, T)
+        gather(words_g[0], words[0], 0, S)
+        interleave(3, 0, 512, 352)
+        interleave(3, 512, 1024, 832)
+        quantize(1, 0, 512)
+        quantize(1, 512, 1024)
+        interleave(4, 0, 512, 272)
+        interleave(4, 512, 768, 640)
+        quantize(1, 1024, 1536)
+        interleave(5, 0, 256, 96)
+        quantize(1, 1536, 1792)
+        quantize(1, 1792, T)
+        gather(words_g[1], words[1], 0, S)
+        gather(planes_g, planes, 0, 256)
+        expert(0)
+        gather(planes_g, planes, 256, S)
+        for e in range(1, E):
+            expert(e)
+        for lo, hi in ((0, 256), (256, 512), (512, S)):
+            scatter(lo, hi)
+        nc.sync.dma_start(out=out, in_=out_sb[:])

@@ -61,15 +61,6 @@ def tile_moe_two_lin_relu_kernel(
         nc.gpsimd.memset(w_planes[:].bitcast(I32), 0)
         nc.gpsimd.memset(planes[:].bitcast(I32), 0)
         nc.vector.memset(out_sb[:], 0.0)
-        for q in range(4):
-            nc.gpsimd.dma_start(
-                out=w_planes[32 * q + 4 : 32 * q + 8].bitcast(I32),
-                in_=w8_scales[:, :, 4 * q : 4 * q + 4, :].rearrange("e a q n -> q (e a) n").bitcast(I32),
-            )
-            nc.gpsimd.dma_start(
-                out=w_planes[32 * q : 32 * q + 4].bitcast(I32),
-                in_=w4_scales[:, :, 4 * q : 4 * q + 4, :].rearrange("e a q n -> q (e a) n").bitcast(I32),
-            )
 
         raws = []
         for i, (a, c0, width) in enumerate(LOADS):
@@ -81,6 +72,15 @@ def tile_moe_two_lin_relu_kernel(
                 nc.sync.dma_start(offs_sb[:], offs)
         nc.sync.dma_start(out=w8_sb[:].bitcast(I32), in_=w8_words.rearrange("e a p n r -> p (e a) (n r)").bitcast(I32))
         nc.sync.dma_start(out=w4_sb[:].bitcast(I32), in_=w4_words.rearrange("e a p n -> p (e a) n").bitcast(I32))
+        for q in range(4):
+            nc.sync.dma_start(
+                out=w_planes[32 * q + 4 : 32 * q + 8].bitcast(I32),
+                in_=w8_scales[:, :, 4 * q : 4 * q + 4, :].rearrange("e a q n -> q (e a) n").bitcast(I32),
+            )
+            nc.sync.dma_start(
+                out=w_planes[32 * q : 32 * q + 4].bitcast(I32),
+                in_=w4_scales[:, :, 4 * q : 4 * q + 4, :].rearrange("e a q n -> q (e a) n").bitcast(I32),
+            )
         nc.sync.dma_start(out=bias[:], in_=b)
         nc.sync.dma_start(dst_sb[:], dst)
         nc.sync.dma_start(out=gate_sb[:], in_=gate)

@@ -24,14 +24,14 @@ PACK = 4
 K_PASS = P * PACK
 PIECE = 512
 LOADS = (
-    (0, 0, 1024),
-    (0, 1024, 512),
-    (0, 1536, 512),
-    (1, 0, 1024),
-    (1, 1024, 768),
+    (0, 0, 1280),
+    (0, 1280, 768),
+    (1, 0, 1152),
+    (1, 1152, 640),
     (1, 1792, 256),
 )
 PLANE_ROW = (4, 0)
+TAIL = ((0, 256), (256, 768), (768, S))
 
 
 def tile_moe_two_lin_relu_kernel(
@@ -86,17 +86,14 @@ def tile_moe_two_lin_relu_kernel(
         nc.sync.dma_start(out=gate_sb[:], in_=gate)
         acts = keep.tile([P, S], F32, name="acts")
 
-        def interleave(i, lo, hi, cut):
+        def interleave(i, lo, hi, on_scalar):
             a, c0, width = LOADS[i]
-            for first, last, on_scalar in ((lo, cut, True), (cut, hi, False)):
-                if first == last:
-                    continue
-                to = grouped[a][:, c0 + first : c0 + last, :].rearrange("p (c i) j -> p c j i", i=4)
-                source = raws[i][:, :, first:last].rearrange("p j (c i) -> p c j i", i=4)
-                if on_scalar:
-                    nc.scalar.activation(to, source, COPY)
-                else:
-                    nc.vector.tensor_copy(out=to, in_=source)
+            to = grouped[a][:, lo:hi, :].rearrange("p (c i) j -> p c j i", i=4)
+            source = raws[i][:, :, lo - c0 : hi - c0].rearrange("p j (c i) -> p c j i", i=4)
+            if on_scalar:
+                nc.scalar.activation(to, source, COPY)
+            else:
+                nc.vector.tensor_copy(out=to, in_=source)
 
         def quantize(a, lo, hi):
             nc.vector.quantize_mx(
@@ -137,32 +134,46 @@ def tile_moe_two_lin_relu_kernel(
                 out_sb[:].indirect(dst_sb[:, lo // 16 : hi // 16]), acts[:, lo:hi], gate_sb[:, lo:hi], MULT
             )
 
-        interleave(0, 0, 512, 256)
-        interleave(0, 512, 1024, 768)
-        quantize(0, 0, 512)
-        quantize(0, 512, 1024)
-        interleave(1, 0, 512, 256)
-        quantize(0, 1024, 1536)
-        interleave(2, 0, 256, 96)
-        interleave(2, 256, 512, 352)
-        quantize(0, 1536, T)
+        interleave(0, 0, 256, True)
+        interleave(0, 256, 512, True)
+        interleave(0, 512, 640, True)
+        interleave(0, 768, 1280, False)
+        interleave(0, 640, 768, False)
+        quantize(0, 768, 1280)
+        quantize(0, 0, 256)
+        quantize(0, 256, 512)
+        quantize(0, 512, 768)
+        interleave(1, 1280, 1536, True)
+        interleave(1, 1536, 1600, True)
+        interleave(1, 1792, 2048, False)
+        interleave(1, 1600, 1792, False)
+        quantize(0, 1792, 2048)
+        quantize(0, 1280, 1536)
+        quantize(0, 1536, 1792)
         gather(words_g[0], words[0], 0, S)
-        interleave(3, 0, 512, 352)
-        interleave(3, 512, 1024, 832)
-        quantize(1, 0, 512)
-        quantize(1, 512, 1024)
-        interleave(4, 0, 512, 272)
-        interleave(4, 512, 768, 640)
-        quantize(1, 1024, 1536)
-        interleave(5, 0, 256, 96)
+        interleave(2, 0, 256, True)
+        interleave(2, 256, 512, True)
+        interleave(2, 512, 640, True)
+        interleave(2, 640, 1152, False)
+        quantize(1, 0, 256)
+        quantize(1, 640, 1152)
+        quantize(1, 256, 512)
+        quantize(1, 512, 640)
+        interleave(3, 1152, 1408, True)
+        interleave(3, 1408, 1472, True)
+        interleave(3, 1536, 1792, False)
+        interleave(3, 1472, 1536, False)
         quantize(1, 1536, 1792)
+        quantize(1, 1152, 1408)
+        quantize(1, 1408, 1536)
+        interleave(4, 1792, 1920, True)
+        interleave(4, 1920, 2048, False)
         quantize(1, 1792, T)
         gather(words_g[1], words[1], 0, S)
-        gather(planes_g, planes, 0, 256)
-        expert(0)
-        gather(planes_g, planes, 256, S)
-        for e in range(1, E):
-            expert(e)
-        for lo, hi in ((0, 256), (256, 512), (512, S)):
+        for lo, hi in TAIL:
+            gather(planes_g, planes, lo, hi)
+            for e in range(lo // C, hi // C):
+                expert(e)
+        for lo, hi in TAIL:
             scatter(lo, hi)
         nc.sync.dma_start(out=out, in_=out_sb[:])

@@ -24,10 +24,11 @@ PACK = 4
 K_PASS = P * PACK
 PIECE = 512
 LOADS = (
-    (0, 0, 1280),
-    (0, 1280, 768),
-    (1, 0, 1152),
-    (1, 1152, 640),
+    (0, 0, 1152),
+    (0, 1152, 896),
+    (1, 0, 640),
+    (1, 640, 640),
+    (1, 1280, 512),
     (1, 1792, 256),
 )
 PLANE_ROW = (4, 0)
@@ -136,38 +137,30 @@ def tile_moe_two_lin_relu_kernel(
 
         interleave(0, 0, 256, True)
         interleave(0, 256, 512, True)
-        interleave(0, 512, 640, True)
-        interleave(0, 768, 1280, False)
-        interleave(0, 640, 768, False)
-        quantize(0, 768, 1280)
+        interleave(0, 512, 1152, False)
         quantize(0, 0, 256)
+        quantize(0, 640, 1152)
+        quantize(0, 512, 640)
         quantize(0, 256, 512)
-        quantize(0, 512, 768)
-        interleave(1, 1280, 1536, True)
-        interleave(1, 1536, 1600, True)
-        interleave(1, 1792, 2048, False)
-        interleave(1, 1600, 1792, False)
-        quantize(0, 1792, 2048)
-        quantize(0, 1280, 1536)
-        quantize(0, 1536, 1792)
+        interleave(1, 1152, 1408, True)
+        interleave(1, 1408, 1536, True)
+        interleave(1, 1536, 2048, False)
+        quantize(0, 1152, 1408)
+        quantize(0, 1536, 2048)
+        quantize(0, 1408, 1536)
         gather(words_g[0], words[0], 0, S)
-        interleave(2, 0, 256, True)
-        interleave(2, 256, 512, True)
-        interleave(2, 512, 640, True)
-        interleave(2, 640, 1152, False)
-        quantize(1, 0, 256)
-        quantize(1, 640, 1152)
-        quantize(1, 256, 512)
-        quantize(1, 512, 640)
-        interleave(3, 1152, 1408, True)
-        interleave(3, 1408, 1472, True)
-        interleave(3, 1536, 1792, False)
-        interleave(3, 1472, 1536, False)
+        interleave(2, 0, 640, True)
+        interleave(3, 640, 1024, True)
+        interleave(3, 1024, 1280, False)
+        quantize(1, 0, 512)
+        quantize(1, 1024, 1280)
+        quantize(1, 512, 1024)
+        interleave(4, 1280, 1536, True)
+        interleave(4, 1536, 1792, False)
+        quantize(1, 1280, 1536)
+        interleave(5, 1792, 1920, True)
+        interleave(5, 1920, 2048, False)
         quantize(1, 1536, 1792)
-        quantize(1, 1152, 1408)
-        quantize(1, 1408, 1536)
-        interleave(4, 1792, 1920, True)
-        interleave(4, 1920, 2048, False)
         quantize(1, 1792, T)
         gather(words_g[1], words[1], 0, S)
         for lo, hi in TAIL:

@@ -32,7 +32,7 @@ LOADS = (
     (1, 1792, 256),
 )
 PLANE_ROW = (4, 0)
-TAIL = ((0, 256), (256, 768), (768, S))
+TAIL = ((0, 768), (768, S))
 
 
 def tile_moe_two_lin_relu_kernel(
@@ -71,9 +71,8 @@ def tile_moe_two_lin_relu_kernel(
             raws.append(raw)
             if i == 0:
                 nc.sync.dma_start(offs_sb[:], offs)
-        nc.sync.dma_start(out=w8_sb[:].bitcast(I32), in_=w8_words.rearrange("e a p n r -> p (e a) (n r)").bitcast(I32))
-        nc.sync.dma_start(out=w4_sb[:].bitcast(I32), in_=w4_words.rearrange("e a p n -> p (e a) n").bitcast(I32))
-        for q in range(4):
+
+        def load_scales(q):
             nc.sync.dma_start(
                 out=w_planes[32 * q + 4 : 32 * q + 8].bitcast(I32),
                 in_=w8_scales[:, :, 4 * q : 4 * q + 4, :].rearrange("e a q n -> q (e a) n").bitcast(I32),
@@ -82,6 +81,12 @@ def tile_moe_two_lin_relu_kernel(
                 out=w_planes[32 * q : 32 * q + 4].bitcast(I32),
                 in_=w4_scales[:, :, 4 * q : 4 * q + 4, :].rearrange("e a q n -> q (e a) n").bitcast(I32),
             )
+
+        for q in range(3):
+            load_scales(q)
+        nc.sync.dma_start(out=w8_sb[:].bitcast(I32), in_=w8_words.rearrange("e a p n r -> p (e a) (n r)").bitcast(I32))
+        nc.sync.dma_start(out=w4_sb[:].bitcast(I32), in_=w4_words.rearrange("e a p n -> p (e a) n").bitcast(I32))
+        load_scales(3)
         nc.sync.dma_start(out=bias[:], in_=b)
         nc.sync.dma_start(dst_sb[:], dst)
         nc.sync.dma_start(out=gate_sb[:], in_=gate)
@@ -162,9 +167,9 @@ def tile_moe_two_lin_relu_kernel(
         interleave(5, 1920, 2048, False)
         quantize(1, 1536, 1792)
         quantize(1, 1792, T)
-        gather(words_g[1], words[1], 0, S)
         for lo, hi in TAIL:
             gather(planes_g, planes, lo, hi)
+            gather(words_g[1], words[1], lo, hi)
             for e in range(lo // C, hi // C):
                 expert(e)
         for lo, hi in TAIL:

@@ -32,7 +32,7 @@ LOADS = (
     (1, 1792, 256),
 )
 PLANE_ROW = (4, 0)
-TAIL = ((0, 768), (768, S))
+TAIL = ((0, 512), (512, S))
 
 
 def tile_moe_two_lin_relu_kernel(
@@ -113,17 +113,18 @@ def tile_moe_two_lin_relu_kernel(
 
         def expert(e):
             acc = psum.tile([P, C], F32, name="acc")
+            own = slice(e * C, (e + 1) * C)
+            nc.tensor.matmul_mx(
+                out=acc[:],
+                lhsT=w8_sb[:, e, :].bitcast(E4M3X4),
+                lhsT_scale=w_planes[PLANE_ROW[0] : P, e, :],
+                rhs=words_g[0][:, own].bitcast(E4M3X4),
+                rhs_scale=planes_g[PLANE_ROW[0] : P, own],
+                start=True,
+                stop=False,
+            )
             for h in range(0, C, 128):
                 cols = slice(e * C + h, e * C + h + 128)
-                nc.tensor.matmul_mx(
-                    out=acc[:, h : h + 128],
-                    lhsT=w8_sb[:, e, :].bitcast(E4M3X4),
-                    lhsT_scale=w_planes[PLANE_ROW[0] : P, e, :],
-                    rhs=words_g[0][:, cols].bitcast(E4M3X4),
-                    rhs_scale=planes_g[PLANE_ROW[0] : P, cols],
-                    start=True,
-                    stop=False,
-                )
                 nc.tensor.matmul_mx(
                     out=acc[:, h : h + 128],
                     lhsT=w4_sb[:, e, :].bitcast(E2M1X4),
@@ -131,7 +132,7 @@ def tile_moe_two_lin_relu_kernel(
                     rhs=words_g[1][:, cols].bitcast(E4M3X4),
                     rhs_scale=planes_g[PLANE_ROW[1] : P, cols],
                     start=False,
-                    stop=True,
+                    stop=(h + 128 == C),
                 )
             nc.scalar.activation(acts[:, e * C : (e + 1) * C], acc[:], RELU, bias=bias[:, e : e + 1])
 
@@ -167,11 +168,12 @@ def tile_moe_two_lin_relu_kernel(
         interleave(5, 1920, 2048, False)
         quantize(1, 1536, 1792)
         quantize(1, 1792, T)
+        gather(planes_g, planes, 0, S)
         for lo, hi in TAIL:
-            gather(planes_g, planes, lo, hi)
             gather(words_g[1], words[1], lo, hi)
             for e in range(lo // C, hi // C):
                 expert(e)
         for lo, hi in TAIL:
             scatter(lo, hi)
-        nc.sync.dma_start(out=out, in_=out_sb[:])
+        nc.sync.dma_start(out=out[:, : T // 2], in_=out_sb[:, : T // 2])
+        nc.scalar.dma_start(out=out[:, T // 2 :], in_=out_sb[:, T // 2 :])

@@ -22,17 +22,9 @@ FLOPS = 2 * K * N * S
 P = 128
 PACK = 4
 K_PASS = P * PACK
+HALF = T // 2
 PIECE = 512
-LOADS = (
-    (0, 0, 1152),
-    (0, 1152, 896),
-    (1, 0, 640),
-    (1, 640, 640),
-    (1, 1280, 512),
-    (1, 1792, 256),
-)
-PLANE_ROW = (4, 0)
-TAIL = ((0, 512), (512, S))
+W_ROW = (4, 0)
 
 
 def tile_moe_two_lin_relu_kernel(
@@ -41,36 +33,37 @@ def tile_moe_two_lin_relu_kernel(
     nc = tc.nc
     with ExitStack() as ctx:
         keep = ctx.enter_context(tc.tile_pool(name="keep", bufs=1))
-        stage = ctx.enter_context(tc.tile_pool(name="stage", bufs=len(LOADS)))
-        work = ctx.enter_context(tc.tile_pool(name="work", bufs=E))
         psum = ctx.enter_context(tc.psum_pool(name="psum", bufs=E))
 
         offs_sb = keep.tile([P, S // 16], U16, name="offs_sb")
         dst_sb = keep.tile([P, S // 16], U16, name="dst_sb")
-        words = [keep.tile([P, T], U32, name=f"words{a}", align_bytes=64) for a in range(2)]
-        planes = keep.tile([P, T], U8, name="planes", align_bytes=64)
-        words_g = [keep.tile([P, S], U32, name=f"words_g{a}", align_bytes=64) for a in range(2)]
-        planes_g = keep.tile([P, S], U8, name="planes_g", align_bytes=64)
-        grouped = [keep.tile([P, T, PACK], BF16, name=f"grouped{a}", align_bytes=64) for a in range(2)]
+        pairs = [keep.tile([P, T], U32, name=f"pairs{u}", align_bytes=64) for u in range(4)]
+        picked = [keep.tile([P, 2, S], U32, name=f"picked{a}", align_bytes=64) for a in range(2)]
+        woven0 = keep.tile([P, 2 * S], U32, name="woven0", align_bytes=64)
+        woven1 = [keep.tile([P, 2 * PIECE], U32, name=f"woven1_{i}", align_bytes=64) for i in range(S // PIECE)]
+        codes = [keep.tile([P, S], U32, name=f"codes{a}", align_bytes=64) for a in range(2)]
+        planes = [keep.tile([P, S], U8, name=f"planes{a}", align_bytes=64) for a in range(2)]
         w8_sb = keep.tile([P, E, 4 * N], U8, name="w8_sb", align_bytes=64)
         w4_sb = keep.tile([P, E, 2 * N], U8, name="w4_sb", align_bytes=64)
         w_planes = keep.tile([P, E, N], U8, name="w_planes", align_bytes=64)
         bias = keep.tile([P, E], F32, name="bias")
         gate_sb = keep.tile([P, S], F32, name="gate_sb")
         out_sb = keep.tile([P, T], F32, name="out_sb")
+        acts = keep.tile([P, S], F32, name="acts")
 
         nc.gpsimd.memset(w_planes[:].bitcast(I32), 0)
-        nc.gpsimd.memset(planes[:].bitcast(I32), 0)
         nc.vector.memset(out_sb[:], 0.0)
 
-        raws = []
-        for i, (a, c0, width) in enumerate(LOADS):
-            raw = keep.tile([P, PACK, width], F32, name=f"raw{i}")
-            rows = xT[a * K_PASS : (a + 1) * K_PASS, c0 : c0 + width]
-            nc.sync.dma_start(out=raw[:], in_=rows.rearrange("(p j) w -> p j w", j=PACK))
-            raws.append(raw)
-            if i == 0:
-                nc.sync.dma_start(offs_sb[:], offs)
+        raws = {}
+        for u in range(4):
+            a, j = u // 2, 2 * (u % 2)
+            rows = xT[a * K_PASS : (a + 1) * K_PASS, :].rearrange("(p j) w -> p j w", j=PACK)
+            for h in range(2):
+                raw = keep.tile([P, 2, HALF], F32, name=f"raw{u}_{h}")
+                nc.sync.dma_start(out=raw[:], in_=rows[:, j : j + 2, h * HALF : (h + 1) * HALF])
+                raws[u, h] = raw
+                if (u, h) == (0, 0):
+                    nc.sync.dma_start(offs_sb[:], offs)
 
         def load_scales(q):
             nc.sync.dma_start(
@@ -90,90 +83,94 @@ def tile_moe_two_lin_relu_kernel(
         nc.sync.dma_start(out=bias[:], in_=b)
         nc.sync.dma_start(dst_sb[:], dst)
         nc.sync.dma_start(out=gate_sb[:], in_=gate)
-        acts = keep.tile([P, S], F32, name="acts")
 
-        def interleave(i, lo, hi, on_scalar):
-            a, c0, width = LOADS[i]
-            to = grouped[a][:, lo:hi, :].rearrange("p (c i) j -> p c j i", i=4)
-            source = raws[i][:, :, lo - c0 : hi - c0].rearrange("p j (c i) -> p c j i", i=4)
+        def cast(u, lo, hi, on_scalar):
+            h = lo // HALF
+            to = pairs[u][:, lo:hi].bitcast(BF16).rearrange("p (c i j) -> p c j i", i=4, j=2)
+            source = raws[u, h][:, :, lo - h * HALF : hi - h * HALF].rearrange("p j (c i) -> p c j i", i=4)
             if on_scalar:
                 nc.scalar.activation(to, source, COPY)
             else:
                 nc.vector.tensor_copy(out=to, in_=source)
 
-        def quantize(a, lo, hi):
-            nc.vector.quantize_mx(
-                out=words[a][:, lo:hi].bitcast(E4M3X4),
-                scales=planes[PLANE_ROW[a] : P, lo:hi],
-                in_=grouped[a][:, lo:hi, :].rearrange("p c j -> p (c j)"),
-            )
+        def gather(u, lo, hi):
+            nc.vector.tensor_copy(picked[u // 2][:, u % 2, lo:hi], pairs[u][:].indirect(offs_sb[:, lo // 16 : hi // 16]))
 
-        def gather(target, source, lo, hi):
-            nc.vector.tensor_copy(target[:, lo:hi], source[:].indirect(offs_sb[:, lo // 16 : hi // 16]))
+        def weave(to, a, lo, hi, on_scalar):
+            kind = U32 if on_scalar else I32
+            to = to.bitcast(kind).rearrange("p (c i u) -> p c u i", i=2, u=2)
+            source = picked[a][:, :, lo:hi].bitcast(kind).rearrange("p u (c i) -> p c u i", i=2)
+            if on_scalar:
+                nc.scalar.copy(to, source)
+            else:
+                nc.vector.tensor_copy(out=to, in_=source)
 
-        def expert(e):
-            acc = psum.tile([P, C], F32, name="acc")
+        def quantize(a, lo, hi, woven):
+            nc.vector.quantize_mx(out=codes[a][:, lo:hi].bitcast(E4M3X4), scales=planes[a][:, lo:hi], in_=woven.bitcast(BF16))
+
+        accs = [psum.tile([P, C], F32, name="acc") for e in range(E)]
+
+        def first_pass(e):
             own = slice(e * C, (e + 1) * C)
             nc.tensor.matmul_mx(
-                out=acc[:],
+                out=accs[e][:],
                 lhsT=w8_sb[:, e, :].bitcast(E4M3X4),
-                lhsT_scale=w_planes[PLANE_ROW[0] : P, e, :],
-                rhs=words_g[0][:, own].bitcast(E4M3X4),
-                rhs_scale=planes_g[PLANE_ROW[0] : P, own],
+                lhsT_scale=w_planes[W_ROW[0] : P, e, :],
+                rhs=codes[0][:, own].bitcast(E4M3X4),
+                rhs_scale=planes[0][:, own],
                 start=True,
                 stop=False,
             )
+
+        def second_pass(e):
             for h in range(0, C, 128):
                 cols = slice(e * C + h, e * C + h + 128)
                 nc.tensor.matmul_mx(
-                    out=acc[:, h : h + 128],
+                    out=accs[e][:, h : h + 128],
                     lhsT=w4_sb[:, e, :].bitcast(E2M1X4),
-                    lhsT_scale=w_planes[PLANE_ROW[1] : P, e, :],
-                    rhs=words_g[1][:, cols].bitcast(E4M3X4),
-                    rhs_scale=planes_g[PLANE_ROW[1] : P, cols],
+                    lhsT_scale=w_planes[W_ROW[1] : P, e, :],
+                    rhs=codes[1][:, cols].bitcast(E4M3X4),
+                    rhs_scale=planes[1][:, cols],
                     start=False,
                     stop=(h + 128 == C),
                 )
-            nc.scalar.activation(acts[:, e * C : (e + 1) * C], acc[:], RELU, bias=bias[:, e : e + 1])
+
+        def relu(e):
+            nc.scalar.activation(acts[:, e * C : (e + 1) * C], accs[e][:], RELU, bias=bias[:, e : e + 1])
 
         def scatter(lo, hi):
             nc.vector.tensor_tensor(
                 out_sb[:].indirect(dst_sb[:, lo // 16 : hi // 16]), acts[:, lo:hi], gate_sb[:, lo:hi], MULT
             )
 
-        interleave(0, 0, 256, True)
-        interleave(0, 256, 512, True)
-        interleave(0, 512, 1152, False)
-        quantize(0, 0, 256)
-        quantize(0, 640, 1152)
-        quantize(0, 512, 640)
-        quantize(0, 256, 512)
-        interleave(1, 1152, 1408, True)
-        interleave(1, 1408, 1536, True)
-        interleave(1, 1536, 2048, False)
-        quantize(0, 1152, 1408)
-        quantize(0, 1536, 2048)
-        quantize(0, 1408, 1536)
-        gather(words_g[0], words[0], 0, S)
-        interleave(2, 0, 640, True)
-        interleave(3, 640, 1024, True)
-        interleave(3, 1024, 1280, False)
-        quantize(1, 0, 512)
-        quantize(1, 1024, 1280)
-        quantize(1, 512, 1024)
-        interleave(4, 1280, 1536, True)
-        interleave(4, 1536, 1792, False)
-        quantize(1, 1280, 1536)
-        interleave(5, 1792, 1920, True)
-        interleave(5, 1920, 2048, False)
-        quantize(1, 1536, 1792)
-        quantize(1, 1792, T)
-        gather(planes_g, planes, 0, S)
-        for lo, hi in TAIL:
-            gather(words_g[1], words[1], lo, hi)
-            for e in range(lo // C, hi // C):
-                expert(e)
-        for lo, hi in TAIL:
-            scatter(lo, hi)
+        for h in range(2):
+            cast(0, h * HALF, h * HALF + 352, True)
+            cast(0, h * HALF + 352, (h + 1) * HALF, False)
+        gather(0, 0, S)
+        cast(1, 0, HALF, True)
+        cast(1, HALF, HALF + 256, True)
+        cast(1, HALF + 256, T, False)
+        gather(1, 0, S)
+        weave(woven0[:], 0, 0, S, False)
+        quantize(0, 0, 1024, woven0[:, :2048])
+        quantize(0, 1024, S, woven0[:, 2048:])
+        for e in range(E):
+            first_pass(e)
+        cast(2, 0, HALF, True)
+        cast(2, HALF, T, True)
+        gather(2, 0, S)
+        cast(3, 0, HALF, True)
+        cast(3, HALF, T, True)
+        for i in range(S // PIECE):
+            gather(3, i * PIECE, (i + 1) * PIECE)
+        for i in range(S // PIECE):
+            weave(woven1[i][:], 1, i * PIECE, (i + 1) * PIECE, True)
+        for i in range(S // PIECE):
+            quantize(1, i * PIECE, (i + 1) * PIECE, woven1[i][:])
+        for e in range(E):
+            second_pass(e)
+            relu(e)
+        scatter(0, PIECE)
+        scatter(PIECE, S)
         nc.sync.dma_start(out=out[:, : T // 2], in_=out_sb[:, : T // 2])
         nc.scalar.dma_start(out=out[:, T // 2 :], in_=out_sb[:, T // 2 :])

@@ -16,6 +16,7 @@ E2M1X4 = mybir.dt.float4_e2m1fn_x4
 COPY = mybir.ActivationFunctionType.Copy
 RELU = mybir.ActivationFunctionType.Relu
 MULT = mybir.AluOpType.mult
+ADD = mybir.AluOpType.add
 
 FLOPS = 2 * K * N * S
 
@@ -37,7 +38,7 @@ def tile_moe_two_lin_relu_kernel(
 
         offs_sb = keep.tile([P, S // 16], U16, name="offs_sb")
         dst_sb = keep.tile([P, S // 16], U16, name="dst_sb")
-        pairs = [keep.tile([P, T], U32, name=f"pairs{u}", align_bytes=64) for u in range(4)]
+        pairs = [keep.tile([P, T], U32, name=f"pairs{u}", align_bytes=64) for u in range(3)]
         picked = [keep.tile([P, 2, S], U32, name=f"picked{a}", align_bytes=64) for a in range(2)]
         woven0 = keep.tile([P, 2 * S], U32, name="woven0", align_bytes=64)
         woven1 = [keep.tile([P, 2 * PIECE], U32, name=f"woven1_{i}", align_bytes=64) for i in range(S // PIECE)]
@@ -59,7 +60,7 @@ def tile_moe_two_lin_relu_kernel(
             a, j = u // 2, 2 * (u % 2)
             rows = xT[a * K_PASS : (a + 1) * K_PASS, :].rearrange("(p j) w -> p j w", j=PACK)
             for h in range(2):
-                raw = keep.tile([P, 2, HALF], F32, name=f"raw{u}_{h}")
+                raw = keep.tile([P, 2, HALF], F32, name=f"raw{u}_{h}", tag=f"raw{u}_{h}", align_bytes=64)
                 nc.sync.dma_start(out=raw[:], in_=rows[:, j : j + 2, h * HALF : (h + 1) * HALF])
                 raws[u, h] = raw
                 if (u, h) == (0, 0):
@@ -84,12 +85,14 @@ def tile_moe_two_lin_relu_kernel(
         nc.sync.dma_start(dst_sb[:], dst)
         nc.sync.dma_start(out=gate_sb[:], in_=gate)
 
-        def cast(u, lo, hi, on_scalar):
+        def cast(u, lo, hi, engine):
             h = lo // HALF
             to = pairs[u][:, lo:hi].bitcast(BF16).rearrange("p (c i j) -> p c j i", i=4, j=2)
             source = raws[u, h][:, :, lo - h * HALF : hi - h * HALF].rearrange("p j (c i) -> p c j i", i=4)
-            if on_scalar:
+            if engine == "scalar":
                 nc.scalar.activation(to, source, COPY)
+            elif engine == "gpsimd":
+                nc.gpsimd.tensor_scalar(to, source, 1.0, 0.0, MULT, ADD)
             else:
                 nc.vector.tensor_copy(out=to, in_=source)
 
@@ -144,23 +147,27 @@ def tile_moe_two_lin_relu_kernel(
             )
 
         for h in range(2):
-            cast(0, h * HALF, h * HALF + 352, True)
-            cast(0, h * HALF + 352, (h + 1) * HALF, False)
+            cast(0, h * HALF, h * HALF + 352, "scalar")
+            cast(0, h * HALF + 352, (h + 1) * HALF, "vector")
         gather(0, 0, S)
-        cast(1, 0, HALF, True)
-        cast(1, HALF, HALF + 256, True)
-        cast(1, HALF + 256, T, False)
-        gather(1, 0, S)
-        weave(woven0[:], 0, 0, S, False)
-        quantize(0, 0, 1024, woven0[:, :2048])
-        quantize(0, 1024, S, woven0[:, 2048:])
+        cast(1, 0, HALF, "scalar")
+        cast(1, HALF, HALF + 320, "scalar")
+        cast(1, HALF + 320, T, "vector")
+        for i in range(S // PIECE):
+            gather(1, i * PIECE, (i + 1) * PIECE)
+        for i in range(S // PIECE):
+            weave(woven0[:, 2 * i * PIECE : 2 * (i + 1) * PIECE], 0, i * PIECE, (i + 1) * PIECE, i < 2)
+        cast(2, 0, 832, "gpsimd")
+        cast(2, 832, HALF, "scalar")
+        quantize(0, 0, 2 * PIECE, woven0[:, : 4 * PIECE])
+        quantize(0, 2 * PIECE, S, woven0[:, 4 * PIECE :])
         for e in range(E):
             first_pass(e)
-        cast(2, 0, HALF, True)
-        cast(2, HALF, T, True)
+        cast(2, HALF, T, "scalar")
         gather(2, 0, S)
-        cast(3, 0, HALF, True)
-        cast(3, HALF, T, True)
+        pairs.append(keep.tile([P, T], U32, name="pairs3", tag="raw2_1", align_bytes=64))
+        cast(3, 0, HALF, "gpsimd")
+        cast(3, HALF, T, "scalar")
         for i in range(S // PIECE):
             gather(3, i * PIECE, (i + 1) * PIECE)
         for i in range(S // PIECE):

@@ -34,15 +34,21 @@ def tile_moe_two_lin_relu_kernel(
     nc = tc.nc
     with ExitStack() as ctx:
         keep = ctx.enter_context(tc.tile_pool(name="keep", bufs=1))
+        shared = ctx.enter_context(tc.tile_pool(name="shared", bufs=1))
         psum = ctx.enter_context(tc.psum_pool(name="psum", bufs=E))
 
         offs_sb = keep.tile([P, S // 16], U16, name="offs_sb")
         dst_sb = keep.tile([P, S // 16], U16, name="dst_sb")
         pairs = [keep.tile([P, T], U32, name=f"pairs{u}", align_bytes=64) for u in range(3)]
         picked = [keep.tile([P, 2, S], U32, name=f"picked{a}", align_bytes=64) for a in range(2)]
-        woven0 = keep.tile([P, 2 * S], U32, name="woven0", align_bytes=64)
-        woven1 = [keep.tile([P, 2 * PIECE], U32, name=f"woven1_{i}", align_bytes=64) for i in range(S // PIECE)]
-        codes = [keep.tile([P, S], U32, name=f"codes{a}", align_bytes=64) for a in range(2)]
+        woven0 = [keep.tile([P, 2 * PIECE], U32, name=f"woven0_{i}", align_bytes=64) for i in range(2)]
+        woven1 = [keep.tile([P, 2 * PIECE], U32, name=f"woven1_{i}", tag=f"woven1_{i}", align_bytes=64) for i in range(S // PIECE)]
+        codes = {
+            (a, i): keep.tile([P, PIECE], U32, name=f"codes{a}_{i}", align_bytes=64)
+            for a in range(2)
+            for i in range(S // PIECE)
+            if (a, i) != (0, 2)
+        }
         planes = [keep.tile([P, S], U8, name=f"planes{a}", align_bytes=64) for a in range(2)]
         w8_sb = keep.tile([P, E, 4 * N], U8, name="w8_sb", align_bytes=64)
         w4_sb = keep.tile([P, E, 2 * N], U8, name="w4_sb", align_bytes=64)
@@ -60,7 +66,10 @@ def tile_moe_two_lin_relu_kernel(
             a, j = u // 2, 2 * (u % 2)
             rows = xT[a * K_PASS : (a + 1) * K_PASS, :].rearrange("(p j) w -> p j w", j=PACK)
             for h in range(2):
-                raw = keep.tile([P, 2, HALF], F32, name=f"raw{u}_{h}", tag=f"raw{u}_{h}", align_bytes=64)
+                if (u, h) == (2, 1):
+                    raw = shared.tile([P, 2, HALF], F32, name="raw2_1", align_bytes=64, offset=2048)
+                else:
+                    raw = keep.tile([P, 2, HALF], F32, name=f"raw{u}_{h}")
                 nc.sync.dma_start(out=raw[:], in_=rows[:, j : j + 2, h * HALF : (h + 1) * HALF])
                 raws[u, h] = raw
                 if (u, h) == (0, 0):
@@ -108,8 +117,12 @@ def tile_moe_two_lin_relu_kernel(
             else:
                 nc.vector.tensor_copy(out=to, in_=source)
 
-        def quantize(a, lo, hi, woven):
-            nc.vector.quantize_mx(out=codes[a][:, lo:hi].bitcast(E4M3X4), scales=planes[a][:, lo:hi], in_=woven.bitcast(BF16))
+        def quantize(a, i, woven):
+            nc.vector.quantize_mx(
+                out=codes[a, i][:].bitcast(E4M3X4),
+                scales=planes[a][:, i * PIECE : (i + 1) * PIECE],
+                in_=woven[:].bitcast(BF16),
+            )
 
         accs = [psum.tile([P, C], F32, name="acc") for e in range(E)]
 
@@ -119,7 +132,7 @@ def tile_moe_two_lin_relu_kernel(
                 out=accs[e][:],
                 lhsT=w8_sb[:, e, :].bitcast(E4M3X4),
                 lhsT_scale=w_planes[W_ROW[0] : P, e, :],
-                rhs=codes[0][:, own].bitcast(E4M3X4),
+                rhs=codes[0, e // 2][:, e % 2 * C : (e % 2 + 1) * C].bitcast(E4M3X4),
                 rhs_scale=planes[0][:, own],
                 start=True,
                 stop=False,
@@ -132,7 +145,7 @@ def tile_moe_two_lin_relu_kernel(
                     out=accs[e][:, h : h + 128],
                     lhsT=w4_sb[:, e, :].bitcast(E2M1X4),
                     lhsT_scale=w_planes[W_ROW[1] : P, e, :],
-                    rhs=codes[1][:, cols].bitcast(E4M3X4),
+                    rhs=codes[1, e // 2][:, e % 2 * C + h : e % 2 * C + h + 128].bitcast(E4M3X4),
                     rhs_scale=planes[1][:, cols],
                     start=False,
                     stop=(h + 128 == C),
@@ -155,26 +168,36 @@ def tile_moe_two_lin_relu_kernel(
         cast(1, HALF + 320, T, "vector")
         for i in range(S // PIECE):
             gather(1, i * PIECE, (i + 1) * PIECE)
-        for i in range(S // PIECE):
-            weave(woven0[:, 2 * i * PIECE : 2 * (i + 1) * PIECE], 0, i * PIECE, (i + 1) * PIECE, i < 2)
-        cast(2, 0, 832, "gpsimd")
-        cast(2, 832, HALF, "scalar")
-        quantize(0, 0, 2 * PIECE, woven0[:, : 4 * PIECE])
-        quantize(0, 2 * PIECE, S, woven0[:, 4 * PIECE :])
-        for e in range(E):
+        for i in range(2):
+            weave(woven0[i][:], 0, i * PIECE, (i + 1) * PIECE, True)
+        cast(2, 0, 768, "gpsimd")
+        cast(2, 768, HALF, "scalar")
+        for i in range(2):
+            quantize(0, i, woven0[i])
+        for e in range(4):
             first_pass(e)
-        cast(2, HALF, T, "scalar")
+        cast(2, HALF, T - 416, "scalar")
+        cast(2, T - 416, T, "vector")
         gather(2, 0, S)
-        pairs.append(keep.tile([P, T], U32, name="pairs3", tag="raw2_1", align_bytes=64))
-        cast(3, 0, HALF, "gpsimd")
-        cast(3, HALF, T, "scalar")
+        late = shared.tile([P, 2 * PIECE], U32, name="woven0_2", align_bytes=64, offset=0)
+        pairs.append(shared.tile([P, T], U32, name="pairs3", align_bytes=64, offset=4096))
+        weave(late[:], 0, 2 * PIECE, S, True)
+        cast(3, 0, 640, "gpsimd")
+        cast(3, 640, HALF, "scalar")
+        cast(3, HALF, HALF + 448, "gpsimd")
+        cast(3, HALF + 448, T, "scalar")
         for i in range(S // PIECE):
             gather(3, i * PIECE, (i + 1) * PIECE)
         for i in range(S // PIECE):
             weave(woven1[i][:], 1, i * PIECE, (i + 1) * PIECE, True)
-        for i in range(S // PIECE):
-            quantize(1, i * PIECE, (i + 1) * PIECE, woven1[i][:])
+        quantize(1, 0, woven1[0])
+        codes[0, 2] = keep.tile([P, PIECE], U32, name="codes0_2", tag="woven1_0", align_bytes=64)
+        quantize(0, 2, late)
+        quantize(1, 1, woven1[1])
+        quantize(1, 2, woven1[2])
         for e in range(E):
+            if e >= 4:
+                first_pass(e)
             second_pass(e)
             relu(e)
         scatter(0, PIECE)

@@ -23,7 +23,7 @@ FLOPS = 2 * K * N * S
 P = 128
 PACK = 4
 K_PASS = P * PACK
-HALF = T // 2
+CUTS = ((0, 1280, T), (0, 1280, T), (0, 1024, T), (0, 1024, 1536, T))
 PIECE = 512
 W_ROW = (4, 0)
 
@@ -34,7 +34,6 @@ def tile_moe_two_lin_relu_kernel(
     nc = tc.nc
     with ExitStack() as ctx:
         keep = ctx.enter_context(tc.tile_pool(name="keep", bufs=1))
-        shared = ctx.enter_context(tc.tile_pool(name="shared", bufs=1))
         psum = ctx.enter_context(tc.psum_pool(name="psum", bufs=E))
 
         offs_sb = keep.tile([P, S // 16], U16, name="offs_sb")
@@ -65,14 +64,11 @@ def tile_moe_two_lin_relu_kernel(
         for u in range(4):
             a, j = u // 2, 2 * (u % 2)
             rows = xT[a * K_PASS : (a + 1) * K_PASS, :].rearrange("(p j) w -> p j w", j=PACK)
-            for h in range(2):
-                if (u, h) == (2, 1):
-                    raw = shared.tile([P, 2, HALF], F32, name="raw2_1", align_bytes=64, offset=2048)
-                else:
-                    raw = keep.tile([P, 2, HALF], F32, name=f"raw{u}_{h}")
-                nc.sync.dma_start(out=raw[:], in_=rows[:, j : j + 2, h * HALF : (h + 1) * HALF])
-                raws[u, h] = raw
-                if (u, h) == (0, 0):
+            for lo, hi in zip(CUTS[u], CUTS[u][1:]):
+                raw = keep.tile([P, 2, hi - lo], F32, name=f"raw{u}_{lo}", tag=f"raw{u}_{lo}", align_bytes=64)
+                nc.sync.dma_start(out=raw[:], in_=rows[:, j : j + 2, lo:hi])
+                raws[u, lo] = raw
+                if (u, lo) == (0, 0):
                     nc.sync.dma_start(offs_sb[:], offs)
 
         def load_scales(q):
@@ -95,9 +91,9 @@ def tile_moe_two_lin_relu_kernel(
         nc.sync.dma_start(out=gate_sb[:], in_=gate)
 
         def cast(u, lo, hi, engine):
-            h = lo // HALF
+            first = max(c for c in CUTS[u] if c <= lo)
             to = pairs[u][:, lo:hi].bitcast(BF16).rearrange("p (c i j) -> p c j i", i=4, j=2)
-            source = raws[u, h][:, :, lo - h * HALF : hi - h * HALF].rearrange("p j (c i) -> p c j i", i=4)
+            source = raws[u, first][:, :, lo - first : hi - first].rearrange("p j (c i) -> p c j i", i=4)
             if engine == "scalar":
                 nc.scalar.activation(to, source, COPY)
             elif engine == "gpsimd":
@@ -159,33 +155,36 @@ def tile_moe_two_lin_relu_kernel(
                 out_sb[:].indirect(dst_sb[:, lo // 16 : hi // 16]), acts[:, lo:hi], gate_sb[:, lo:hi], MULT
             )
 
-        for h in range(2):
-            cast(0, h * HALF, h * HALF + 352, "scalar")
-            cast(0, h * HALF + 352, (h + 1) * HALF, "vector")
+        cast(0, 0, 512, "scalar")
+        cast(0, 512, 1280, "vector")
+        cast(0, 1280, 1536, "scalar")
+        cast(0, 1536, T, "vector")
         gather(0, 0, S)
-        cast(1, 0, HALF, "scalar")
-        cast(1, HALF, HALF + 320, "scalar")
-        cast(1, HALF + 320, T, "vector")
+        cast(1, 0, 512, "gpsimd")
+        cast(1, 512, 1280, "scalar")
+        cast(1, 1280, 1568, "scalar")
+        cast(1, 1568, T, "vector")
         for i in range(S // PIECE):
             gather(1, i * PIECE, (i + 1) * PIECE)
-        for i in range(2):
-            weave(woven0[i][:], 0, i * PIECE, (i + 1) * PIECE, True)
+        weave(woven0[0][:], 0, 0, PIECE, True)
         cast(2, 0, 768, "gpsimd")
-        cast(2, 768, HALF, "scalar")
+        cast(2, 768, 1024, "scalar")
+        weave(woven0[1][:], 0, PIECE, 2 * PIECE, True)
         for i in range(2):
             quantize(0, i, woven0[i])
         for e in range(4):
             first_pass(e)
-        cast(2, HALF, T - 416, "scalar")
-        cast(2, T - 416, T, "vector")
+        cast(2, 1024, T - 352, "scalar")
+        cast(2, T - 352, T, "vector")
         gather(2, 0, S)
-        late = shared.tile([P, 2 * PIECE], U32, name="woven0_2", align_bytes=64, offset=0)
-        pairs.append(shared.tile([P, T], U32, name="pairs3", align_bytes=64, offset=4096))
+        pairs.append(keep.tile([P, T], U32, name="pairs3", tag="raw2_1024", align_bytes=64))
+        cast(3, 0, 448, "gpsimd")
+        cast(3, 448, 1024, "scalar")
+        cast(3, 1024, 1536, "scalar")
+        cast(3, 1536, 1760, "gpsimd")
+        cast(3, 1760, T, "scalar")
+        late = keep.tile([P, 2 * PIECE], U32, name="woven0_2", tag="raw3_1536", align_bytes=64)
         weave(late[:], 0, 2 * PIECE, S, True)
-        cast(3, 0, 640, "gpsimd")
-        cast(3, 640, HALF, "scalar")
-        cast(3, HALF, HALF + 448, "gpsimd")
-        cast(3, HALF + 448, T, "scalar")
         for i in range(S // PIECE):
             gather(3, i * PIECE, (i + 1) * PIECE)
         for i in range(S // PIECE):

@@ -23,7 +23,7 @@ FLOPS = 2 * K * N * S
 P = 128
 PACK = 4
 K_PASS = P * PACK
-CUTS = ((0, 1280, T), (0, 1280, T), (0, 1024, T), (0, 1024, 1536, T))
+CUTS = ((0, 1024, T), (0, 1024, 1536, T), (0, 1024, T), (0, 1024, 1536, T))
 PIECE = 512
 W_ROW = (4, 0)
 
@@ -155,15 +155,16 @@ def tile_moe_two_lin_relu_kernel(
                 out_sb[:].indirect(dst_sb[:, lo // 16 : hi // 16]), acts[:, lo:hi], gate_sb[:, lo:hi], MULT
             )
 
-        cast(0, 0, 512, "scalar")
-        cast(0, 512, 1280, "vector")
-        cast(0, 1280, 1536, "scalar")
-        cast(0, 1536, T, "vector")
+        for lo in (0, 1024):
+            cast(0, lo, lo + 384, "scalar")
+            cast(0, lo + 384, lo + 1024, "vector")
         gather(0, 0, S)
-        cast(1, 0, 512, "gpsimd")
-        cast(1, 512, 1280, "scalar")
-        cast(1, 1280, 1568, "scalar")
-        cast(1, 1568, T, "vector")
+        cast(1, 0, 448, "gpsimd")
+        cast(1, 448, 1024, "scalar")
+        cast(1, 1024, 1216, "gpsimd")
+        cast(1, 1216, 1536, "scalar")
+        cast(1, 1536, 1760, "scalar")
+        cast(1, 1760, T, "vector")
         for i in range(S // PIECE):
             gather(1, i * PIECE, (i + 1) * PIECE)
         weave(woven0[0][:], 0, 0, PIECE, True)
@@ -174,8 +175,8 @@ def tile_moe_two_lin_relu_kernel(
             quantize(0, i, woven0[i])
         for e in range(4):
             first_pass(e)
-        cast(2, 1024, T - 352, "scalar")
-        cast(2, T - 352, T, "vector")
+        cast(2, 1024, T - 448, "scalar")
+        cast(2, T - 448, T, "vector")
         gather(2, 0, S)
         pairs.append(keep.tile([P, T], U32, name="pairs3", tag="raw2_1024", align_bytes=64))
         cast(3, 0, 448, "gpsimd")

@@ -23,7 +23,7 @@ FLOPS = 2 * K * N * S
 P = 128
 PACK = 4
 K_PASS = P * PACK
-CUTS = ((0, 1024, T), (0, 1024, 1536, T), (0, 1024, T), (0, 1024, 1536, T))
+CUTS = ((0, 1024, T), (0, 1024, 1536, T), (0, 1024, T), (0, 1024, 1664, T))
 PIECE = 512
 W_ROW = (4, 0)
 
@@ -168,23 +168,24 @@ def tile_moe_two_lin_relu_kernel(
         for i in range(S // PIECE):
             gather(1, i * PIECE, (i + 1) * PIECE)
         weave(woven0[0][:], 0, 0, PIECE, True)
-        cast(2, 0, 768, "gpsimd")
-        cast(2, 768, 1024, "scalar")
+        cast(2, 0, 896, "gpsimd")
+        cast(2, 896, 1024, "scalar")
         weave(woven0[1][:], 0, PIECE, 2 * PIECE, True)
         for i in range(2):
             quantize(0, i, woven0[i])
         for e in range(4):
             first_pass(e)
-        cast(2, 1024, T - 448, "scalar")
-        cast(2, T - 448, T, "vector")
+        cast(2, 1024, T - 400, "scalar")
+        cast(2, T - 400, T, "vector")
         gather(2, 0, S)
         pairs.append(keep.tile([P, T], U32, name="pairs3", tag="raw2_1024", align_bytes=64))
         cast(3, 0, 448, "gpsimd")
         cast(3, 448, 1024, "scalar")
-        cast(3, 1024, 1536, "scalar")
-        cast(3, 1536, 1760, "gpsimd")
-        cast(3, 1760, T, "scalar")
-        late = keep.tile([P, 2 * PIECE], U32, name="woven0_2", tag="raw3_1536", align_bytes=64)
+        cast(3, 1024, 1280, "gpsimd")
+        cast(3, 1280, 1664, "scalar")
+        cast(3, 1664, 1808, "gpsimd")
+        cast(3, 1808, T, "scalar")
+        late = keep.tile([P, 2 * PIECE], U32, name="woven0_2", tag="raw3_1664", align_bytes=64)
         weave(late[:], 0, 2 * PIECE, S, True)
         for i in range(S // PIECE):
             gather(3, i * PIECE, (i + 1) * PIECE)

@@ -23,7 +23,7 @@ FLOPS = 2 * K * N * S
 P = 128
 PACK = 4
 K_PASS = P * PACK
-CUTS = ((0, 1024, T), (0, 1024, 1536, T), (0, 1024, T), (0, 1024, 1664, T))
+CUTS = ((0, 1024, T), (0, 1024, 1664, T), (0, 1024, T), (0, 1024, 1664, T))
 PIECE = 512
 W_ROW = (4, 0)
 
@@ -161,22 +161,21 @@ def tile_moe_two_lin_relu_kernel(
         gather(0, 0, S)
         cast(1, 0, 448, "gpsimd")
         cast(1, 448, 1024, "scalar")
-        cast(1, 1024, 1216, "gpsimd")
-        cast(1, 1216, 1536, "scalar")
-        cast(1, 1536, 1760, "scalar")
-        cast(1, 1760, T, "vector")
+        cast(1, 1024, 1248, "gpsimd")
+        cast(1, 1248, 1664, "scalar")
+        cast(1, 1664, 1824, "scalar")
+        cast(1, 1824, T, "vector")
         for i in range(S // PIECE):
             gather(1, i * PIECE, (i + 1) * PIECE)
         weave(woven0[0][:], 0, 0, PIECE, True)
-        cast(2, 0, 896, "gpsimd")
-        cast(2, 896, 1024, "scalar")
+        cast(2, 0, 1024, "gpsimd")
         weave(woven0[1][:], 0, PIECE, 2 * PIECE, True)
         for i in range(2):
             quantize(0, i, woven0[i])
         for e in range(4):
             first_pass(e)
-        cast(2, 1024, T - 400, "scalar")
-        cast(2, T - 400, T, "vector")
+        cast(2, 1024, T - 336, "scalar")
+        cast(2, T - 336, T, "vector")
         gather(2, 0, S)
         pairs.append(keep.tile([P, T], U32, name="pairs3", tag="raw2_1024", align_bytes=64))
         cast(3, 0, 448, "gpsimd")

@@ -23,7 +23,7 @@ FLOPS = 2 * K * N * S
 P = 128
 PACK = 4
 K_PASS = P * PACK
-CUTS = ((0, 1024, T), (0, 1024, 1664, T), (0, 1024, T), (0, 1024, 1664, T))
+CUTS = ((0, 1024, T), (0, 1024, T), (0, 1024, T), (0, 1024, 1664, T))
 PIECE = 512
 W_ROW = (4, 0)
 
@@ -159,12 +159,9 @@ def tile_moe_two_lin_relu_kernel(
             cast(0, lo, lo + 384, "scalar")
             cast(0, lo + 384, lo + 1024, "vector")
         gather(0, 0, S)
-        cast(1, 0, 448, "gpsimd")
-        cast(1, 448, 1024, "scalar")
-        cast(1, 1024, 1248, "gpsimd")
-        cast(1, 1248, 1664, "scalar")
-        cast(1, 1664, 1824, "scalar")
-        cast(1, 1824, T, "vector")
+        cast(1, 0, 1024, "scalar")
+        cast(1, 1024, 1408, "scalar")
+        cast(1, 1408, T, "vector")
         for i in range(S // PIECE):
             gather(1, i * PIECE, (i + 1) * PIECE)
         weave(woven0[0][:], 0, 0, PIECE, True)

@@ -23,7 +23,7 @@ FLOPS = 2 * K * N * S
 P = 128
 PACK = 4
 K_PASS = P * PACK
-CUTS = ((0, 1024, T), (0, 1024, T), (0, 1024, T), (0, 1024, 1664, T))
+CUTS = ((0, 1024, T), (0, 1280, T), (0, 1024, T), (0, 1024, 1664, T))
 PIECE = 512
 W_ROW = (4, 0)
 
@@ -159,9 +159,10 @@ def tile_moe_two_lin_relu_kernel(
             cast(0, lo, lo + 384, "scalar")
             cast(0, lo + 384, lo + 1024, "vector")
         gather(0, 0, S)
-        cast(1, 0, 1024, "scalar")
-        cast(1, 1024, 1408, "scalar")
-        cast(1, 1408, T, "vector")
+        cast(1, 0, 512, "gpsimd")
+        cast(1, 512, 1280, "scalar")
+        cast(1, 1280, 1568, "scalar")
+        cast(1, 1568, T, "vector")
         for i in range(S // PIECE):
             gather(1, i * PIECE, (i + 1) * PIECE)
         weave(woven0[0][:], 0, 0, PIECE, True)

@@ -23,9 +23,10 @@ FLOPS = 2 * K * N * S
 P = 128
 PACK = 4
 K_PASS = P * PACK
-CUTS = ((0, 1024, T), (0, 1280, T), (0, 1024, T), (0, 1024, 1664, T))
 PIECE = 512
-W_ROW = (4, 0)
+PAIR_CUTS = ((0, 1280, T), (0, 1280, T), (0, 1024, T))
+ROW_CUTS = ((0, 1024, T), (0, 768, 1536, T))
+AHEAD = 3
 
 
 def tile_moe_two_lin_relu_kernel(
@@ -34,66 +35,63 @@ def tile_moe_two_lin_relu_kernel(
     nc = tc.nc
     with ExitStack() as ctx:
         keep = ctx.enter_context(tc.tile_pool(name="keep", bufs=1))
+        reuse = ctx.enter_context(tc.tile_pool(name="reuse", bufs=1))
         psum = ctx.enter_context(tc.psum_pool(name="psum", bufs=E))
 
         offs_sb = keep.tile([P, S // 16], U16, name="offs_sb")
         dst_sb = keep.tile([P, S // 16], U16, name="dst_sb")
         pairs = [keep.tile([P, T], U32, name=f"pairs{u}", align_bytes=64) for u in range(3)]
-        picked = [keep.tile([P, 2, S], U32, name=f"picked{a}", align_bytes=64) for a in range(2)]
-        woven0 = [keep.tile([P, 2 * PIECE], U32, name=f"woven0_{i}", align_bytes=64) for i in range(2)]
-        woven1 = [keep.tile([P, 2 * PIECE], U32, name=f"woven1_{i}", tag=f"woven1_{i}", align_bytes=64) for i in range(S // PIECE)]
-        codes = {
-            (a, i): keep.tile([P, PIECE], U32, name=f"codes{a}_{i}", align_bytes=64)
-            for a in range(2)
-            for i in range(S // PIECE)
-            if (a, i) != (0, 2)
-        }
+        rows16 = [keep.tile([P, T], BF16, name=f"rows16_{r}", align_bytes=64) for r in range(2)]
+        picked = keep.tile([P, 2, S], U32, name="picked", align_bytes=64)
+        woven1 = keep.tile([P, 2 * S], U32, name="woven1", align_bytes=64)
+        codes1 = [keep.tile([P, C], U32, name=f"codes1_{e}", tag=f"codes1_{e}", align_bytes=64) for e in range(E)]
         planes = [keep.tile([P, S], U8, name=f"planes{a}", align_bytes=64) for a in range(2)]
-        w8_sb = keep.tile([P, E, 4 * N], U8, name="w8_sb", align_bytes=64)
-        w4_sb = keep.tile([P, E, 2 * N], U8, name="w4_sb", align_bytes=64)
-        w_planes = keep.tile([P, E, N], U8, name="w_planes", align_bytes=64)
+        w_planes = [keep.tile([P, E, N], U8, name="w8_planes", align_bytes=64)]
         bias = keep.tile([P, E], F32, name="bias")
-        gate_sb = keep.tile([P, S], F32, name="gate_sb")
         out_sb = keep.tile([P, T], F32, name="out_sb")
         acts = keep.tile([P, S], F32, name="acts")
 
-        nc.gpsimd.memset(w_planes[:].bitcast(I32), 0)
+        nc.gpsimd.memset(w_planes[0][:].bitcast(I32), 0)
         nc.vector.memset(out_sb[:], 0.0)
 
+        def load_scales(q, a):
+            scales = (w8_scales, w4_scales)[a]
+            nc.sync.dma_start(
+                out=w_planes[a][32 * q : 32 * q + 4].bitcast(I32),
+                in_=scales[:, :, 4 * q : 4 * q + 4, :].rearrange("e a q n -> q (e a) n").bitcast(I32),
+            )
+
+        by_row = [xT[a * K_PASS : (a + 1) * K_PASS, :].rearrange("(p j) w -> p j w", j=PACK) for a in range(2)]
         raws = {}
-        for u in range(4):
+        place = {}
+        at = 0
+        for u in range(3):
             a, j = u // 2, 2 * (u % 2)
-            rows = xT[a * K_PASS : (a + 1) * K_PASS, :].rearrange("(p j) w -> p j w", j=PACK)
-            for lo, hi in zip(CUTS[u], CUTS[u][1:]):
-                raw = keep.tile([P, 2, hi - lo], F32, name=f"raw{u}_{lo}", tag=f"raw{u}_{lo}", align_bytes=64)
-                nc.sync.dma_start(out=raw[:], in_=rows[:, j : j + 2, lo:hi])
+            for lo, hi in zip(PAIR_CUTS[u], PAIR_CUTS[u][1:]):
+                if (u, hi) == (2, T):
+                    at = at + 8 * PIECE
+                raw = reuse.tile([P, 2, hi - lo], F32, name=f"raw{u}_{lo}", offset=at, align_bytes=64)
+                place[u, lo] = at
+                at = at + 8 * (hi - lo)
+                nc.sync.dma_start(out=raw[:], in_=by_row[a][:, j : j + 2, lo:hi])
                 raws[u, lo] = raw
                 if (u, lo) == (0, 0):
                     nc.sync.dma_start(offs_sb[:], offs)
+                    nc.sync.dma_start(out=bias[:], in_=b)
 
-        def load_scales(q):
-            nc.sync.dma_start(
-                out=w_planes[32 * q + 4 : 32 * q + 8].bitcast(I32),
-                in_=w8_scales[:, :, 4 * q : 4 * q + 4, :].rearrange("e a q n -> q (e a) n").bitcast(I32),
-            )
-            nc.sync.dma_start(
-                out=w_planes[32 * q : 32 * q + 4].bitcast(I32),
-                in_=w4_scales[:, :, 4 * q : 4 * q + 4, :].rearrange("e a q n -> q (e a) n").bitcast(I32),
-            )
+        def load_row(r, at):
+            for lo, hi in zip(ROW_CUTS[r], ROW_CUTS[r][1:]):
+                raw = reuse.tile([P, hi - lo], F32, name=f"row{r}_{lo}", offset=at + 4 * lo, align_bytes=64)
+                place[3 + r, lo] = at + 4 * lo
+                nc.sync.dma_start(out=raw[:], in_=by_row[1][:, 2 + r, lo:hi])
+                raws[3 + r, lo] = raw
 
-        for q in range(3):
-            load_scales(q)
-        nc.sync.dma_start(out=w8_sb[:].bitcast(I32), in_=w8_words.rearrange("e a p n r -> p (e a) (n r)").bitcast(I32))
-        nc.sync.dma_start(out=w4_sb[:].bitcast(I32), in_=w4_words.rearrange("e a p n -> p (e a) n").bitcast(I32))
-        load_scales(3)
-        nc.sync.dma_start(out=bias[:], in_=b)
+        load_row(0, at)
         nc.sync.dma_start(dst_sb[:], dst)
-        nc.sync.dma_start(out=gate_sb[:], in_=gate)
+        for q in range(4):
+            load_scales(q, 0)
 
-        def cast(u, lo, hi, engine):
-            first = max(c for c in CUTS[u] if c <= lo)
-            to = pairs[u][:, lo:hi].bitcast(BF16).rearrange("p (c i j) -> p c j i", i=4, j=2)
-            source = raws[u, first][:, :, lo - first : hi - first].rearrange("p j (c i) -> p c j i", i=4)
+        def round_on(engine, to, source):
             if engine == "scalar":
                 nc.scalar.activation(to, source, COPY)
             elif engine == "gpsimd":
@@ -101,23 +99,49 @@ def tile_moe_two_lin_relu_kernel(
             else:
                 nc.vector.tensor_copy(out=to, in_=source)
 
+        def cast(u, lo, hi, engine):
+            first = max(c for c in PAIR_CUTS[u] if c <= lo)
+            to = pairs[u][:, lo:hi].bitcast(BF16).rearrange("p (c i j) -> p c j i", i=4, j=2)
+            source = raws[u, first][:, :, lo - first : hi - first].rearrange("p j (c i) -> p c j i", i=4)
+            round_on(engine, to, source)
+
+        def cast_row(r, lo, hi, engine):
+            first = max(c for c in ROW_CUTS[r] if c <= lo)
+            round_on(engine, rows16[r][:, lo:hi], raws[3 + r, first][:, lo - first : hi - first])
+
+        def listed(lo, hi):
+            return offs_sb[:, lo // 16 : hi // 16]
+
         def gather(u, lo, hi):
-            nc.vector.tensor_copy(picked[u // 2][:, u % 2, lo:hi], pairs[u][:].indirect(offs_sb[:, lo // 16 : hi // 16]))
+            nc.vector.tensor_copy(picked[:, u, lo:hi], pairs[u][:].indirect(listed(lo, hi)))
 
-        def weave(to, a, lo, hi, on_scalar):
-            kind = U32 if on_scalar else I32
-            to = to.bitcast(kind).rearrange("p (c i u) -> p c u i", i=2, u=2)
-            source = picked[a][:, :, lo:hi].bitcast(kind).rearrange("p u (c i) -> p c u i", i=2)
-            if on_scalar:
-                nc.scalar.copy(to, source)
-            else:
-                nc.vector.tensor_copy(out=to, in_=source)
+        def gather_stepped(lo, hi):
+            to = woven1[:, 2 * lo : 2 * hi].rearrange("p (s u) -> p s u", u=2)[:, :, 0]
+            nc.vector.tensor_copy(to, pairs[2][:].indirect(listed(lo, hi)))
 
-        def quantize(a, i, woven):
+        def gather_row(r, e):
+            to = woven1[:, 2 * e * C : 2 * (e + 1) * C].bitcast(BF16).rearrange("p (s j) -> p s j", j=PACK)[:, :, 2 + r]
+            nc.scalar.activation(to, rows16[r][:].indirect(listed(e * C, (e + 1) * C)), COPY)
+
+        def weave(to, lo, hi):
+            to = to.rearrange("p (c i u) -> p c u i", i=2, u=2)
+            nc.scalar.copy(to, picked[:, :, lo:hi].rearrange("p u (c i) -> p c u i", i=2))
+
+        codes0 = {}
+
+        def quantize0(i, woven, codes):
+            codes0[i] = codes
             nc.vector.quantize_mx(
-                out=codes[a, i][:].bitcast(E4M3X4),
-                scales=planes[a][:, i * PIECE : (i + 1) * PIECE],
+                out=codes0[i][:].bitcast(E4M3X4),
+                scales=planes[0][:, i * PIECE : (i + 1) * PIECE],
                 in_=woven[:].bitcast(BF16),
+            )
+
+        def quantize1(e):
+            nc.vector.quantize_mx(
+                out=codes1[e][:].bitcast(E4M3X4),
+                scales=planes[1][:, e * C : (e + 1) * C],
+                in_=woven1[:, 2 * e * C : 2 * (e + 1) * C].bitcast(BF16),
             )
 
         accs = [psum.tile([P, C], F32, name="acc") for e in range(E)]
@@ -127,8 +151,8 @@ def tile_moe_two_lin_relu_kernel(
             nc.tensor.matmul_mx(
                 out=accs[e][:],
                 lhsT=w8_sb[:, e, :].bitcast(E4M3X4),
-                lhsT_scale=w_planes[W_ROW[0] : P, e, :],
-                rhs=codes[0, e // 2][:, e % 2 * C : (e % 2 + 1) * C].bitcast(E4M3X4),
+                lhsT_scale=w_planes[0][:, e, :],
+                rhs=codes0[e // 2][:, e % 2 * C : (e % 2 + 1) * C].bitcast(E4M3X4),
                 rhs_scale=planes[0][:, own],
                 start=True,
                 stop=False,
@@ -136,28 +160,37 @@ def tile_moe_two_lin_relu_kernel(
 
         def second_pass(e):
             for h in range(0, C, 128):
-                cols = slice(e * C + h, e * C + h + 128)
                 nc.tensor.matmul_mx(
                     out=accs[e][:, h : h + 128],
                     lhsT=w4_sb[:, e, :].bitcast(E2M1X4),
-                    lhsT_scale=w_planes[W_ROW[1] : P, e, :],
-                    rhs=codes[1, e // 2][:, e % 2 * C + h : e % 2 * C + h + 128].bitcast(E4M3X4),
-                    rhs_scale=planes[1][:, cols],
+                    lhsT_scale=w_planes[1][:, e, :],
+                    rhs=codes1[e][:, h : h + 128].bitcast(E4M3X4),
+                    rhs_scale=planes[1][:, e * C + h : e * C + h + 128],
                     start=False,
                     stop=(h + 128 == C),
                 )
 
+        parked = woven1[:].bitcast(F32)
+
+        def bias_of(e):
+            if e + AHEAD < E:
+                at = 2 * (e + AHEAD) * C + 1
+                return parked[:, at : at + 1]
+            return bias[:, e : e + 1]
+
         def relu(e):
-            nc.scalar.activation(acts[:, e * C : (e + 1) * C], accs[e][:], RELU, bias=bias[:, e : e + 1])
+            nc.scalar.activation(acts[:, e * C : (e + 1) * C], accs[e][:], RELU, bias=bias_of(e))
 
         def scatter(lo, hi):
             nc.vector.tensor_tensor(
                 out_sb[:].indirect(dst_sb[:, lo // 16 : hi // 16]), acts[:, lo:hi], gate_sb[:, lo:hi], MULT
             )
 
-        for lo in (0, 1024):
-            cast(0, lo, lo + 384, "scalar")
-            cast(0, lo + 384, lo + 1024, "vector")
+        nc.scalar.activation(parked[:, 2 * AHEAD * C + 1 : 2 * S : 2 * C], bias[:, : E - AHEAD], COPY)
+        cast(0, 0, 480, "scalar")
+        cast(0, 480, 1280, "vector")
+        cast(0, 1280, 1568, "scalar")
+        cast(0, 1568, T, "vector")
         gather(0, 0, S)
         cast(1, 0, 512, "gpsimd")
         cast(1, 512, 1280, "scalar")
@@ -165,40 +198,74 @@ def tile_moe_two_lin_relu_kernel(
         cast(1, 1568, T, "vector")
         for i in range(S // PIECE):
             gather(1, i * PIECE, (i + 1) * PIECE)
-        weave(woven0[0][:], 0, 0, PIECE, True)
-        cast(2, 0, 1024, "gpsimd")
-        weave(woven0[1][:], 0, PIECE, 2 * PIECE, True)
-        for i in range(2):
-            quantize(0, i, woven0[i])
-        for e in range(4):
-            first_pass(e)
-        cast(2, 1024, T - 336, "scalar")
-        cast(2, T - 336, T, "vector")
-        gather(2, 0, S)
-        pairs.append(keep.tile([P, T], U32, name="pairs3", tag="raw2_1024", align_bytes=64))
-        cast(3, 0, 448, "gpsimd")
-        cast(3, 448, 1024, "scalar")
-        cast(3, 1024, 1280, "gpsimd")
-        cast(3, 1280, 1664, "scalar")
-        cast(3, 1664, 1808, "gpsimd")
-        cast(3, 1808, T, "scalar")
-        late = keep.tile([P, 2 * PIECE], U32, name="woven0_2", tag="raw3_1664", align_bytes=64)
-        weave(late[:], 0, 2 * PIECE, S, True)
-        for i in range(S // PIECE):
-            gather(3, i * PIECE, (i + 1) * PIECE)
-        for i in range(S // PIECE):
-            weave(woven1[i][:], 1, i * PIECE, (i + 1) * PIECE, True)
-        quantize(1, 0, woven1[0])
-        codes[0, 2] = keep.tile([P, PIECE], U32, name="codes0_2", tag="woven1_0", align_bytes=64)
-        quantize(0, 2, late)
-        quantize(1, 1, woven1[1])
-        quantize(1, 2, woven1[2])
-        for e in range(E):
-            if e >= 4:
-                first_pass(e)
+        woven0 = [keep.tile([P, 2 * PIECE], U32, name="woven0_0", align_bytes=64)]
+        weave(woven0[0][:], 0, PIECE)
+        cast(2, 0, 640, "gpsimd")
+        cast(2, 640, 1024, "scalar")
+        load_row(1, place[2, 0])
+        cast(2, 1024, 1344, "scalar")
+        cast(2, 1344, T, "vector")
+        at = place[2, 1024] + 64
+        w8_sb = reuse.tile([P, E, 4 * N], U8, name="w8_sb", offset=at, align_bytes=64)
+        w4_sb = reuse.tile([P, E, 2 * N], U8, name="w4_sb", offset=at + E * 4 * N, align_bytes=64)
+        w_planes.append(reuse.tile([P, E, N], U8, name="w4_planes", offset=at + E * 6 * N, align_bytes=64))
+        nc.sync.dma_start(out=w8_sb[:].bitcast(I32), in_=w8_words.rearrange("e a p n r -> p (e a) (n r)").bitcast(I32))
+        nc.sync.dma_start(out=w4_sb[:].bitcast(I32), in_=w4_words.rearrange("e a p n -> p (e a) n").bitcast(I32))
+        nc.gpsimd.memset(w_planes[1][:].bitcast(I32), 0)
+        for q in range(4):
+            load_scales(q, 1)
+        gather_stepped(0, S)
+        woven0.append(reuse.tile([P, 2 * PIECE], U32, name="woven0_1", offset=place[2, 1024] + 64 - 8 * PIECE, align_bytes=64))
+        weave(woven0[1][:], PIECE, 2 * PIECE)
+        cast_row(0, 0, 768, "gpsimd")
+        cast_row(0, 768, 1024, "scalar")
+        cast_row(0, 1024, 1312, "gpsimd")
+        cast_row(0, 1312, T, "scalar")
+        gate_sb = reuse.tile([P, S], F32, name="gate_sb", offset=place[3, 0], align_bytes=64)
+        nc.sync.dma_start(out=gate_sb[:, :PIECE], in_=gate[:, :PIECE])
+        nc.sync.dma_start(out=gate_sb[:, PIECE:], in_=gate[:, PIECE:])
+        for e in range(AHEAD):
+            gather_row(0, e)
+        cast_row(1, 0, 768, "gpsimd")
+        cast_row(1, 768, 1536, "vector")
+        cast_row(1, 1536, T, "vector")
+        for e in range(AHEAD):
+            gather_row(1, e)
+        quantize0(0, woven0[0], reuse.tile([P, PIECE], U32, name="codes0_0", offset=place[4, 1536], align_bytes=64))
+        first_pass(0)
+        first_pass(1)
+        quantize1(0)
+        second_pass(0)
+        quantize0(1, woven0[1], reuse.tile([P, PIECE], U32, name="codes0_1", offset=place[4, 768], align_bytes=64))
+        quantize1(1)
+        second_pass(1)
+        first_pass(2)
+        first_pass(3)
+        quantize1(2)
+        second_pass(2)
+        relu(0)
+        scatter(0, C)
+        relu(1)
+        scatter(C, 2 * C)
+        gather_row(0, 3)
+        gather_row(1, 3)
+        quantize1(3)
+        second_pass(3)
+        relu(2)
+        scatter(2 * C, 3 * C)
+        woven0.append(keep.tile([P, 2 * PIECE], U32, name="woven0_2", tag="codes1_1", align_bytes=64))
+        weave(woven0[2][:], 2 * PIECE, S)
+        quantize0(2, woven0[2], keep.tile([P, PIECE], U32, name="codes0_2", align_bytes=64))
+        first_pass(4)
+        first_pass(5)
+        for e in (4, 5):
+            gather_row(0, e)
+            gather_row(1, e)
+            quantize1(e)
             second_pass(e)
-            relu(e)
-        scatter(0, PIECE)
-        scatter(PIECE, S)
+            relu(e - 1)
+            scatter((e - 1) * C, e * C)
+        relu(5)
+        scatter(5 * C, S)
         nc.sync.dma_start(out=out[:, : T // 2], in_=out_sb[:, : T // 2])
         nc.scalar.dma_start(out=out[:, T // 2 :], in_=out_sb[:, T // 2 :])

@@ -24,9 +24,11 @@ P = 128
 PACK = 4
 K_PASS = P * PACK
 PIECE = 512
-PAIR_CUTS = ((0, 1280, T), (0, 1280, T), (0, 1024, T))
+PAIR_CUTS = ((0, 1280, T), (0, 768, 1536, T), (0, 1280, T))
 ROW_CUTS = ((0, 1024, T), (0, 768, 1536, T))
 AHEAD = 3
+DIRECT = 2
+R0, R1, R2, R3 = 0, 16384, 22528, 34816
 
 
 def tile_moe_two_lin_relu_kernel(
@@ -42,8 +44,12 @@ def tile_moe_two_lin_relu_kernel(
         dst_sb = keep.tile([P, S // 16], U16, name="dst_sb")
         pairs = [keep.tile([P, T], U32, name=f"pairs{u}", align_bytes=64) for u in range(3)]
         rows16 = [keep.tile([P, T], BF16, name=f"rows16_{r}", align_bytes=64) for r in range(2)]
-        picked = keep.tile([P, 2, S], U32, name="picked", align_bytes=64)
-        woven1 = keep.tile([P, 2 * S], U32, name="woven1", align_bytes=64)
+        picked = keep.tile([P, 2, 2 * PIECE], U32, name="picked", align_bytes=64)
+        first1 = keep.tile([P, 2 * DIRECT * C], U32, name="first1", align_bytes=64)
+        rest1 = keep.tile([P, 2 * (S - DIRECT * C)], U32, name="rest1", align_bytes=64)
+        picked1 = {e: rest1[:, 2 * (e - DIRECT) * C : 2 * (e - DIRECT + 1) * C] for e in range(DIRECT, E)}
+        woven1 = {e: first1[:, 2 * e * C : 2 * (e + 1) * C] for e in range(DIRECT)}
+        last0 = keep.tile([P, 2 * PIECE], U32, name="last0", align_bytes=64)
         codes1 = [keep.tile([P, C], U32, name=f"codes1_{e}", tag=f"codes1_{e}", align_bytes=64) for e in range(E)]
         planes = [keep.tile([P, S], U8, name=f"planes{a}", align_bytes=64) for a in range(2)]
         w_planes = [keep.tile([P, E, N], U8, name="w8_planes", align_bytes=64)]
@@ -63,30 +69,24 @@ def tile_moe_two_lin_relu_kernel(
 
         by_row = [xT[a * K_PASS : (a + 1) * K_PASS, :].rearrange("(p j) w -> p j w", j=PACK) for a in range(2)]
         raws = {}
-        place = {}
-        at = 0
-        for u in range(3):
-            a, j = u // 2, 2 * (u % 2)
-            for lo, hi in zip(PAIR_CUTS[u], PAIR_CUTS[u][1:]):
-                if (u, hi) == (2, T):
-                    at = at + 8 * PIECE
-                raw = reuse.tile([P, 2, hi - lo], F32, name=f"raw{u}_{lo}", offset=at, align_bytes=64)
-                place[u, lo] = at
-                at = at + 8 * (hi - lo)
-                nc.sync.dma_start(out=raw[:], in_=by_row[a][:, j : j + 2, lo:hi])
-                raws[u, lo] = raw
-                if (u, lo) == (0, 0):
-                    nc.sync.dma_start(offs_sb[:], offs)
-                    nc.sync.dma_start(out=bias[:], in_=b)
 
-        def load_row(r, at):
-            for lo, hi in zip(ROW_CUTS[r], ROW_CUTS[r][1:]):
-                raw = reuse.tile([P, hi - lo], F32, name=f"row{r}_{lo}", offset=at + 4 * lo, align_bytes=64)
-                place[3 + r, lo] = at + 4 * lo
-                nc.sync.dma_start(out=raw[:], in_=by_row[1][:, 2 + r, lo:hi])
-                raws[3 + r, lo] = raw
+        def load_pair(u, lo, hi, at):
+            raw = reuse.tile([P, 2, hi - lo], F32, name=f"raw{u}_{lo}", offset=at, align_bytes=64)
+            nc.sync.dma_start(out=raw[:], in_=by_row[u // 2][:, 2 * (u % 2) : 2 * (u % 2) + 2, lo:hi])
+            raws[u, lo] = raw
 
-        load_row(0, at)
+        def load_piece(r, lo, hi, at):
+            raw = reuse.tile([P, hi - lo], F32, name=f"row{r}_{lo}", offset=at, align_bytes=64)
+            nc.sync.dma_start(out=raw[:], in_=by_row[1][:, 2 + r, lo:hi])
+            raws[3 + r, lo] = raw
+
+        load_pair(0, 0, 1280, R0)
+        nc.sync.dma_start(offs_sb[:], offs)
+        nc.sync.dma_start(out=bias[:], in_=b)
+        load_pair(0, 1280, T, R1)
+        load_pair(1, 0, 768, R2)
+        load_pair(1, 768, 1536, R2 + 6144)
+        load_pair(1, 1536, T, R3)
         nc.sync.dma_start(dst_sb[:], dst)
         for q in range(4):
             load_scales(q, 0)
@@ -115,13 +115,28 @@ def tile_moe_two_lin_relu_kernel(
         def gather(u, lo, hi):
             nc.vector.tensor_copy(picked[:, u, lo:hi], pairs[u][:].indirect(listed(lo, hi)))
 
-        def gather_stepped(lo, hi):
-            to = woven1[:, 2 * lo : 2 * hi].rearrange("p (s u) -> p s u", u=2)[:, :, 0]
-            nc.vector.tensor_copy(to, pairs[2][:].indirect(listed(lo, hi)))
+        def gather_woven(u):
+            to = last0[:].rearrange("p (s u) -> p s u", u=2)[:, :, u]
+            nc.vector.tensor_copy(to, pairs[u][:].indirect(listed(2 * PIECE, S)))
+
+        def gather_third():
+            to = first1[:].rearrange("p (s u) -> p s u", u=2)[:, :, 0]
+            nc.vector.tensor_copy(to, pairs[2][:].indirect(listed(0, DIRECT * C)))
+            to = rest1[:].rearrange("p (e u c) -> p e u c", u=2, c=C)[:, :, 0, :]
+            nc.vector.tensor_copy(to, pairs[2][:].indirect(listed(DIRECT * C, S)))
 
         def gather_row(r, e):
-            to = woven1[:, 2 * e * C : 2 * (e + 1) * C].bitcast(BF16).rearrange("p (s j) -> p s j", j=PACK)[:, :, 2 + r]
+            if e < DIRECT:
+                to = woven1[e].bitcast(BF16).rearrange("p (s j) -> p s j", j=PACK)[:, :, 2 + r]
+            else:
+                to = picked1[e][:, C:].bitcast(BF16).rearrange("p (s j) -> p s j", j=2)[:, :, r]
             nc.scalar.activation(to, rows16[r][:].indirect(listed(e * C, (e + 1) * C)), COPY)
+
+        def weave1(e, tag):
+            woven = keep.tile([P, 2 * C], U32, name=f"woven1_{e}", tag=tag, align_bytes=64)
+            woven1[e] = woven[:]
+            to = woven[:].rearrange("p (c i u) -> p c u i", i=2, u=2)
+            nc.scalar.copy(to, picked1[e].rearrange("p (u c i) -> p c u i", u=2, i=2))
 
         def weave(to, lo, hi):
             to = to.rearrange("p (c i u) -> p c u i", i=2, u=2)
@@ -141,7 +156,7 @@ def tile_moe_two_lin_relu_kernel(
             nc.vector.quantize_mx(
                 out=codes1[e][:].bitcast(E4M3X4),
                 scales=planes[1][:, e * C : (e + 1) * C],
-                in_=woven1[:, 2 * e * C : 2 * (e + 1) * C].bitcast(BF16),
+                in_=woven1[e].bitcast(BF16),
             )
 
         accs = [psum.tile([P, C], F32, name="acc") for e in range(E)]
@@ -170,11 +185,11 @@ def tile_moe_two_lin_relu_kernel(
                     stop=(h + 128 == C),
                 )
 
-        parked = woven1[:].bitcast(F32)
+        parked = rest1[:].bitcast(F32)
 
         def bias_of(e):
             if e + AHEAD < E:
-                at = 2 * (e + AHEAD) * C + 1
+                at = (2 * (e + AHEAD - DIRECT) + 1) * C
                 return parked[:, at : at + 1]
             return bias[:, e : e + 1]
 
@@ -186,86 +201,86 @@ def tile_moe_two_lin_relu_kernel(
                 out_sb[:].indirect(dst_sb[:, lo // 16 : hi // 16]), acts[:, lo:hi], gate_sb[:, lo:hi], MULT
             )
 
-        nc.scalar.activation(parked[:, 2 * AHEAD * C + 1 : 2 * S : 2 * C], bias[:, : E - AHEAD], COPY)
+        nc.scalar.activation(parked[:, (2 * (AHEAD - DIRECT) + 1) * C : 2 * (S - DIRECT * C) : 2 * C], bias[:, : E - AHEAD], COPY)
         cast(0, 0, 480, "scalar")
         cast(0, 480, 1280, "vector")
-        cast(0, 1280, 1568, "scalar")
-        cast(0, 1568, T, "vector")
-        gather(0, 0, S)
-        cast(1, 0, 512, "gpsimd")
-        cast(1, 512, 1280, "scalar")
-        cast(1, 1280, 1568, "scalar")
-        cast(1, 1568, T, "vector")
-        for i in range(S // PIECE):
-            gather(1, i * PIECE, (i + 1) * PIECE)
-        woven0 = [keep.tile([P, 2 * PIECE], U32, name="woven0_0", align_bytes=64)]
-        weave(woven0[0][:], 0, PIECE)
-        cast(2, 0, 640, "gpsimd")
-        cast(2, 640, 1024, "scalar")
-        load_row(1, place[2, 0])
-        cast(2, 1024, 1344, "scalar")
-        cast(2, 1344, T, "vector")
-        at = place[2, 1024] + 64
-        w8_sb = reuse.tile([P, E, 4 * N], U8, name="w8_sb", offset=at, align_bytes=64)
-        w4_sb = reuse.tile([P, E, 2 * N], U8, name="w4_sb", offset=at + E * 4 * N, align_bytes=64)
-        w_planes.append(reuse.tile([P, E, N], U8, name="w4_planes", offset=at + E * 6 * N, align_bytes=64))
-        nc.sync.dma_start(out=w8_sb[:].bitcast(I32), in_=w8_words.rearrange("e a p n r -> p (e a) (n r)").bitcast(I32))
-        nc.sync.dma_start(out=w4_sb[:].bitcast(I32), in_=w4_words.rearrange("e a p n -> p (e a) n").bitcast(I32))
-        nc.gpsimd.memset(w_planes[1][:].bitcast(I32), 0)
+        load_pair(2, 0, 1280, R0 + 768)
+        w_planes.append(reuse.tile([P, E, N], U8, name="w4_planes", offset=R0, align_bytes=64))
+        nc.vector.memset(w_planes[1][:].bitcast(I32), 0)
         for q in range(4):
             load_scales(q, 1)
-        gather_stepped(0, S)
-        woven0.append(reuse.tile([P, 2 * PIECE], U32, name="woven0_1", offset=place[2, 1024] + 64 - 8 * PIECE, align_bytes=64))
+        cast(0, 1280, 1568, "scalar")
+        cast(0, 1568, T, "vector")
+        load_pair(2, 1280, T, R1)
+        gather(0, 0, 2 * PIECE)
+        gather_woven(0)
+        cast(1, 0, 448, "gpsimd")
+        cast(1, 448, 768, "scalar")
+        cast(1, 768, 1088, "gpsimd")
+        cast(1, 1088, 1536, "scalar")
+        load_piece(0, 0, 1024, R2)
+        load_piece(0, 1024, T, R2 + 4096)
+        cast(1, 1536, 1744, "scalar")
+        cast(1, 1744, T, "vector")
+        load_piece(1, 0, 768, R3)
+        gather(1, 0, PIECE)
+        gather(1, PIECE, 2 * PIECE)
+        gather_woven(1)
+        woven0 = [keep.tile([P, 2 * PIECE], U32, name="woven0_0", tag="woven0_0", align_bytes=64)]
+        weave(woven0[0][:], 0, PIECE)
+        cast(2, 0, 640, "gpsimd")
+        cast(2, 640, 1280, "scalar")
+        load_piece(1, 768, 1536, R0 + 9024)
+        load_piece(1, 1536, T, R0 + 2816)
+        cast(2, 1280, 1568, "scalar")
+        cast(2, 1568, T, "vector")
+        at = R1 + 64
+        w8_sb = reuse.tile([P, E, 4 * N], U8, name="w8_sb", offset=at, align_bytes=64)
+        w4_sb = reuse.tile([P, E, 2 * N], U8, name="w4_sb", offset=at + E * 4 * N, align_bytes=64)
+        nc.sync.dma_start(out=w8_sb[:].bitcast(I32), in_=w8_words.rearrange("e a p n r -> p (e a) (n r)").bitcast(I32))
+        nc.sync.dma_start(out=w4_sb[:].bitcast(I32), in_=w4_words.rearrange("e a p n -> p (e a) n").bitcast(I32))
+        gather_third()
+        woven0.append(reuse.tile([P, 2 * PIECE], U32, name="woven0_1", offset=R1 + 64 - 8 * PIECE, align_bytes=64))
         weave(woven0[1][:], PIECE, 2 * PIECE)
-        cast_row(0, 0, 768, "gpsimd")
-        cast_row(0, 768, 1024, "scalar")
-        cast_row(0, 1024, 1312, "gpsimd")
-        cast_row(0, 1312, T, "scalar")
-        gate_sb = reuse.tile([P, S], F32, name="gate_sb", offset=place[3, 0], align_bytes=64)
+        cast_row(0, 0, 1024, "gpsimd")
+        cast_row(0, 1024, 1344, "gpsimd")
+        cast_row(0, 1344, T, "scalar")
+        gate_sb = reuse.tile([P, S], F32, name="gate_sb", offset=R2, align_bytes=64)
         nc.sync.dma_start(out=gate_sb[:, :PIECE], in_=gate[:, :PIECE])
         nc.sync.dma_start(out=gate_sb[:, PIECE:], in_=gate[:, PIECE:])
         for e in range(AHEAD):
             gather_row(0, e)
         cast_row(1, 0, 768, "gpsimd")
-        cast_row(1, 768, 1536, "vector")
+        cast_row(1, 768, 1280, "gpsimd")
+        cast_row(1, 1280, 1536, "vector")
         cast_row(1, 1536, T, "vector")
         for e in range(AHEAD):
             gather_row(1, e)
-        quantize0(0, woven0[0], reuse.tile([P, PIECE], U32, name="codes0_0", offset=place[4, 1536], align_bytes=64))
-        first_pass(0)
-        first_pass(1)
-        quantize1(0)
-        second_pass(0)
-        quantize0(1, woven0[1], reuse.tile([P, PIECE], U32, name="codes0_1", offset=place[4, 768], align_bytes=64))
-        quantize1(1)
-        second_pass(1)
-        first_pass(2)
-        first_pass(3)
-        quantize1(2)
-        second_pass(2)
-        relu(0)
-        scatter(0, C)
-        relu(1)
-        scatter(C, 2 * C)
-        gather_row(0, 3)
-        gather_row(1, 3)
-        quantize1(3)
-        second_pass(3)
-        relu(2)
-        scatter(2 * C, 3 * C)
-        woven0.append(keep.tile([P, 2 * PIECE], U32, name="woven0_2", tag="codes1_1", align_bytes=64))
-        weave(woven0[2][:], 2 * PIECE, S)
-        quantize0(2, woven0[2], keep.tile([P, PIECE], U32, name="codes0_2", align_bytes=64))
-        first_pass(4)
-        first_pass(5)
-        for e in (4, 5):
-            gather_row(0, e)
-            gather_row(1, e)
+        quantize0(0, woven0[0], reuse.tile([P, PIECE], U32, name="codes0_0", offset=R0 + 2816 + 64 - 4 * PIECE, align_bytes=64))
+        quantize0(1, woven0[1], reuse.tile([P, PIECE], U32, name="codes0_1", offset=R0 + 2816 + 64, align_bytes=64))
+        for e in range(4):
+            first_pass(e)
+        for e in range(DIRECT):
             quantize1(e)
             second_pass(e)
-            relu(e - 1)
-            scatter((e - 1) * C, e * C)
-        relu(5)
-        scatter(5 * C, S)
+        quantize0(2, last0, keep.tile([P, PIECE], U32, name="codes0_2", tag="woven0_0", align_bytes=64))
+        relu(0)
+        scatter(0, C)
+        weave1(2, "codes1_0")
+        quantize1(2)
+        second_pass(2)
+        first_pass(4)
+        first_pass(5)
+        for e in range(AHEAD, E):
+            gather_row(0, e)
+            gather_row(1, e)
+            relu(e - 2)
+            scatter((e - 2) * C, (e - 1) * C)
+            weave1(e, f"woven1_{e}")
+            quantize1(e)
+            second_pass(e)
+        for e in (E - 2, E - 1):
+            relu(e)
+            scatter(e * C, (e + 1) * C)
         nc.sync.dma_start(out=out[:, : T // 2], in_=out_sb[:, : T // 2])
         nc.scalar.dma_start(out=out[:, T // 2 :], in_=out_sb[:, T // 2 :])

@@ -28,7 +28,6 @@ PAIR_CUTS = ((0, 1280, T), (0, 768, 1536, T), (0, 1280, T))
 ROW_CUTS = ((0, 1024, T), (0, 768, 1536, T))
 AHEAD = 3
 DIRECT = 2
-R0, R1, R2, R3 = 0, 16384, 22528, 34816
 
 
 def tile_moe_two_lin_relu_kernel(
@@ -38,7 +37,7 @@ def tile_moe_two_lin_relu_kernel(
     with ExitStack() as ctx:
         keep = ctx.enter_context(tc.tile_pool(name="keep", bufs=1))
         reuse = ctx.enter_context(tc.tile_pool(name="reuse", bufs=1))
-        psum = ctx.enter_context(tc.psum_pool(name="psum", bufs=E))
+        psum = ctx.enter_context(tc.psum_pool(name="psum", bufs=4))
 
         offs_sb = keep.tile([P, S // 16], U16, name="offs_sb")
         dst_sb = keep.tile([P, S // 16], U16, name="dst_sb")
@@ -80,13 +79,25 @@ def tile_moe_two_lin_relu_kernel(
             nc.sync.dma_start(out=raw[:], in_=by_row[1][:, 2 + r, lo:hi])
             raws[3 + r, lo] = raw
 
-        load_pair(0, 0, 1280, R0)
-        nc.sync.dma_start(offs_sb[:], offs)
-        nc.sync.dma_start(out=bias[:], in_=b)
-        load_pair(0, 1280, T, R1)
-        load_pair(1, 0, 768, R2)
-        load_pair(1, 768, 1536, R2 + 6144)
-        load_pair(1, 1536, T, R3)
+        place = {}
+        at = 0
+        for u in range(3):
+            for lo, hi in zip(PAIR_CUTS[u], PAIR_CUTS[u][1:]):
+                if (u, hi) == (2, T):
+                    at = at + 8 * PIECE
+                place[u, lo] = at
+                load_pair(u, lo, hi, at)
+                at = at + 8 * (hi - lo)
+                if (u, lo) == (0, 0):
+                    nc.sync.dma_start(offs_sb[:], offs)
+                    nc.sync.dma_start(out=bias[:], in_=b)
+        for r in range(2):
+            for lo, hi in zip(ROW_CUTS[r], ROW_CUTS[r][1:]):
+                if (r, hi) == (1, T):
+                    at = at + 4 * PIECE
+                place[3 + r, lo] = at
+                load_piece(r, lo, hi, at)
+                at = at + 4 * (hi - lo)
         nc.sync.dma_start(dst_sb[:], dst)
         for q in range(4):
             load_scales(q, 0)
@@ -159,10 +170,11 @@ def tile_moe_two_lin_relu_kernel(
                 in_=woven1[e].bitcast(BF16),
             )
 
-        accs = [psum.tile([P, C], F32, name="acc") for e in range(E)]
+        accs = {}
 
         def first_pass(e):
             own = slice(e * C, (e + 1) * C)
+            accs[e] = psum.tile([P, C], F32, name="acc")
             nc.tensor.matmul_mx(
                 out=accs[e][:],
                 lhsT=w8_sb[:, e, :].bitcast(E4M3X4),
@@ -204,25 +216,25 @@ def tile_moe_two_lin_relu_kernel(
         nc.scalar.activation(parked[:, (2 * (AHEAD - DIRECT) + 1) * C : 2 * (S - DIRECT * C) : 2 * C], bias[:, : E - AHEAD], COPY)
         cast(0, 0, 480, "scalar")
         cast(0, 480, 1280, "vector")
-        load_pair(2, 0, 1280, R0 + 768)
-        w_planes.append(reuse.tile([P, E, N], U8, name="w4_planes", offset=R0, align_bytes=64))
+        at = place[0, 0] + E * N
+        w8_sb = reuse.tile([P, E, 4 * N], U8, name="w8_sb", offset=at, align_bytes=64)
+        w4_sb = reuse.tile([P, E, 2 * N], U8, name="w4_sb", offset=at + E * 4 * N, align_bytes=64)
+        nc.sync.dma_start(out=w8_sb[:].bitcast(I32), in_=w8_words.rearrange("e a p n r -> p (e a) (n r)").bitcast(I32))
+        nc.sync.dma_start(out=w4_sb[:].bitcast(I32), in_=w4_words.rearrange("e a p n -> p (e a) n").bitcast(I32))
+        w_planes.append(reuse.tile([P, E, N], U8, name="w4_planes", offset=place[0, 0], align_bytes=64))
         nc.vector.memset(w_planes[1][:].bitcast(I32), 0)
         for q in range(4):
             load_scales(q, 1)
         cast(0, 1280, 1568, "scalar")
         cast(0, 1568, T, "vector")
-        load_pair(2, 1280, T, R1)
         gather(0, 0, 2 * PIECE)
         gather_woven(0)
         cast(1, 0, 448, "gpsimd")
         cast(1, 448, 768, "scalar")
         cast(1, 768, 1088, "gpsimd")
         cast(1, 1088, 1536, "scalar")
-        load_piece(0, 0, 1024, R2)
-        load_piece(0, 1024, T, R2 + 4096)
         cast(1, 1536, 1744, "scalar")
         cast(1, 1744, T, "vector")
-        load_piece(1, 0, 768, R3)
         gather(1, 0, PIECE)
         gather(1, PIECE, 2 * PIECE)
         gather_woven(1)
@@ -230,34 +242,26 @@ def tile_moe_two_lin_relu_kernel(
         weave(woven0[0][:], 0, PIECE)
         cast(2, 0, 640, "gpsimd")
         cast(2, 640, 1280, "scalar")
-        load_piece(1, 768, 1536, R0 + 9024)
-        load_piece(1, 1536, T, R0 + 2816)
         cast(2, 1280, 1568, "scalar")
         cast(2, 1568, T, "vector")
-        at = R1 + 64
-        w8_sb = reuse.tile([P, E, 4 * N], U8, name="w8_sb", offset=at, align_bytes=64)
-        w4_sb = reuse.tile([P, E, 2 * N], U8, name="w4_sb", offset=at + E * 4 * N, align_bytes=64)
-        nc.sync.dma_start(out=w8_sb[:].bitcast(I32), in_=w8_words.rearrange("e a p n r -> p (e a) (n r)").bitcast(I32))
-        nc.sync.dma_start(out=w4_sb[:].bitcast(I32), in_=w4_words.rearrange("e a p n -> p (e a) n").bitcast(I32))
         gather_third()
-        woven0.append(reuse.tile([P, 2 * PIECE], U32, name="woven0_1", offset=R1 + 64 - 8 * PIECE, align_bytes=64))
+        woven0.append(reuse.tile([P, 2 * PIECE], U32, name="woven0_1", offset=place[2, 1280] + 64 - 8 * PIECE, align_bytes=64))
         weave(woven0[1][:], PIECE, 2 * PIECE)
         cast_row(0, 0, 1024, "gpsimd")
         cast_row(0, 1024, 1344, "gpsimd")
         cast_row(0, 1344, T, "scalar")
-        gate_sb = reuse.tile([P, S], F32, name="gate_sb", offset=R2, align_bytes=64)
+        gate_sb = reuse.tile([P, S], F32, name="gate_sb", offset=place[1, 0], align_bytes=64)
         nc.sync.dma_start(out=gate_sb[:, :PIECE], in_=gate[:, :PIECE])
         nc.sync.dma_start(out=gate_sb[:, PIECE:], in_=gate[:, PIECE:])
         for e in range(AHEAD):
             gather_row(0, e)
         cast_row(1, 0, 768, "gpsimd")
-        cast_row(1, 768, 1280, "gpsimd")
-        cast_row(1, 1280, 1536, "vector")
+        cast_row(1, 768, 1536, "gpsimd")
         cast_row(1, 1536, T, "vector")
         for e in range(AHEAD):
             gather_row(1, e)
-        quantize0(0, woven0[0], reuse.tile([P, PIECE], U32, name="codes0_0", offset=R0 + 2816 + 64 - 4 * PIECE, align_bytes=64))
-        quantize0(1, woven0[1], reuse.tile([P, PIECE], U32, name="codes0_1", offset=R0 + 2816 + 64, align_bytes=64))
+        quantize0(0, woven0[0], reuse.tile([P, PIECE], U32, name="codes0_0", offset=place[4, 1536] + 64 - 4 * PIECE, align_bytes=64))
+        quantize0(1, woven0[1], reuse.tile([P, PIECE], U32, name="codes0_1", offset=place[4, 1536] + 64, align_bytes=64))
         for e in range(4):
             first_pass(e)
         for e in range(DIRECT):
@@ -269,8 +273,6 @@ def tile_moe_two_lin_relu_kernel(
         weave1(2, "codes1_0")
         quantize1(2)
         second_pass(2)
-        first_pass(4)
-        first_pass(5)
         for e in range(AHEAD, E):
             gather_row(0, e)
             gather_row(1, e)
@@ -278,6 +280,8 @@ def tile_moe_two_lin_relu_kernel(
             scatter((e - 2) * C, (e - 1) * C)
             weave1(e, f"woven1_{e}")
             quantize1(e)
+            if e >= 4:
+                first_pass(e)
             second_pass(e)
         for e in (E - 2, E - 1):
             relu(e)

@@ -42,7 +42,7 @@ def tile_moe_two_lin_relu_kernel(
         offs_sb = keep.tile([P, S // 16], U16, name="offs_sb")
         dst_sb = keep.tile([P, S // 16], U16, name="dst_sb")
         pairs = [keep.tile([P, T], U32, name=f"pairs{u}", align_bytes=64) for u in range(3)]
-        rows16 = [keep.tile([P, T], BF16, name=f"rows16_{r}", align_bytes=64) for r in range(2)]
+        rows16 = {1: keep.tile([P, T], BF16, name="rows16_1", align_bytes=64)}
         picked = keep.tile([P, 2, 2 * PIECE], U32, name="picked", align_bytes=64)
         first1 = keep.tile([P, 2 * DIRECT * C], U32, name="first1", align_bytes=64)
         rest1 = keep.tile([P, 2 * (S - DIRECT * C)], U32, name="rest1", align_bytes=64)
@@ -91,13 +91,10 @@ def tile_moe_two_lin_relu_kernel(
                 if (u, lo) == (0, 0):
                     nc.sync.dma_start(offs_sb[:], offs)
                     nc.sync.dma_start(out=bias[:], in_=b)
-        for r in range(2):
-            for lo, hi in zip(ROW_CUTS[r], ROW_CUTS[r][1:]):
-                if (r, hi) == (1, T):
-                    at = at + 4 * PIECE
-                place[3 + r, lo] = at
-                load_piece(r, lo, hi, at)
-                at = at + 4 * (hi - lo)
+        at = at + E * 4 * N
+        place[3, 0] = at
+        for lo, hi in zip(ROW_CUTS[0], ROW_CUTS[0][1:]):
+            load_piece(0, lo, hi, at + 4 * lo)
         nc.sync.dma_start(dst_sb[:], dst)
         for q in range(4):
             load_scales(q, 0)
@@ -216,15 +213,6 @@ def tile_moe_two_lin_relu_kernel(
         nc.scalar.activation(parked[:, (2 * (AHEAD - DIRECT) + 1) * C : 2 * (S - DIRECT * C) : 2 * C], bias[:, : E - AHEAD], COPY)
         cast(0, 0, 480, "scalar")
         cast(0, 480, 1280, "vector")
-        at = place[0, 0] + E * N
-        w8_sb = reuse.tile([P, E, 4 * N], U8, name="w8_sb", offset=at, align_bytes=64)
-        w4_sb = reuse.tile([P, E, 2 * N], U8, name="w4_sb", offset=at + E * 4 * N, align_bytes=64)
-        nc.sync.dma_start(out=w8_sb[:].bitcast(I32), in_=w8_words.rearrange("e a p n r -> p (e a) (n r)").bitcast(I32))
-        nc.sync.dma_start(out=w4_sb[:].bitcast(I32), in_=w4_words.rearrange("e a p n -> p (e a) n").bitcast(I32))
-        w_planes.append(reuse.tile([P, E, N], U8, name="w4_planes", offset=place[0, 0], align_bytes=64))
-        nc.vector.memset(w_planes[1][:].bitcast(I32), 0)
-        for q in range(4):
-            load_scales(q, 1)
         cast(0, 1280, 1568, "scalar")
         cast(0, 1568, T, "vector")
         gather(0, 0, 2 * PIECE)
@@ -233,6 +221,8 @@ def tile_moe_two_lin_relu_kernel(
         cast(1, 448, 768, "scalar")
         cast(1, 768, 1088, "gpsimd")
         cast(1, 1088, 1536, "scalar")
+        load_piece(1, 0, 768, place[1, 768])
+        load_piece(1, 768, 1536, place[1, 768] + 4 * 768)
         cast(1, 1536, 1744, "scalar")
         cast(1, 1744, T, "vector")
         gather(1, 0, PIECE)
@@ -242,15 +232,26 @@ def tile_moe_two_lin_relu_kernel(
         weave(woven0[0][:], 0, PIECE)
         cast(2, 0, 640, "gpsimd")
         cast(2, 640, 1280, "scalar")
+        load_piece(1, 1536, T, place[2, 0] + 2816)
+        w_planes.append(reuse.tile([P, E, N], U8, name="w4_planes", offset=place[2, 0], align_bytes=64))
+        nc.gpsimd.memset(w_planes[1][:].bitcast(I32), 0)
+        for q in range(4):
+            load_scales(q, 1)
         cast(2, 1280, 1568, "scalar")
         cast(2, 1568, T, "vector")
+        at = place[2, 1280] + 64
+        w4_sb = reuse.tile([P, E, 2 * N], U8, name="w4_sb", offset=at, align_bytes=64)
+        rows16[0] = reuse.tile([P, T], BF16, name="rows16_0", offset=at + E * 2 * N, align_bytes=64)
+        w8_sb = reuse.tile([P, E, 4 * N], U8, name="w8_sb", offset=at + E * 2 * N + 2 * T, align_bytes=64)
+        nc.sync.dma_start(out=w8_sb[:].bitcast(I32), in_=w8_words.rearrange("e a p n r -> p (e a) (n r)").bitcast(I32))
+        nc.sync.dma_start(out=w4_sb[:].bitcast(I32), in_=w4_words.rearrange("e a p n -> p (e a) n").bitcast(I32))
         gather_third()
         woven0.append(reuse.tile([P, 2 * PIECE], U32, name="woven0_1", offset=place[2, 1280] + 64 - 8 * PIECE, align_bytes=64))
         weave(woven0[1][:], PIECE, 2 * PIECE)
         cast_row(0, 0, 1024, "gpsimd")
         cast_row(0, 1024, 1344, "gpsimd")
         cast_row(0, 1344, T, "scalar")
-        gate_sb = reuse.tile([P, S], F32, name="gate_sb", offset=place[1, 0], align_bytes=64)
+        gate_sb = reuse.tile([P, S], F32, name="gate_sb", offset=place[3, 0], align_bytes=64)
         nc.sync.dma_start(out=gate_sb[:, :PIECE], in_=gate[:, :PIECE])
         nc.sync.dma_start(out=gate_sb[:, PIECE:], in_=gate[:, PIECE:])
         for e in range(AHEAD):
@@ -260,8 +261,8 @@ def tile_moe_two_lin_relu_kernel(
         cast_row(1, 1536, T, "vector")
         for e in range(AHEAD):
             gather_row(1, e)
-        quantize0(0, woven0[0], reuse.tile([P, PIECE], U32, name="codes0_0", offset=place[4, 1536] + 64 - 4 * PIECE, align_bytes=64))
-        quantize0(1, woven0[1], reuse.tile([P, PIECE], U32, name="codes0_1", offset=place[4, 1536] + 64, align_bytes=64))
+        quantize0(0, woven0[0], reuse.tile([P, PIECE], U32, name="codes0_0", offset=place[2, 0] + 2816 + 64 - 4 * PIECE, align_bytes=64))
+        quantize0(1, woven0[1], reuse.tile([P, PIECE], U32, name="codes0_1", offset=place[2, 0] + 2816 + 64, align_bytes=64))
         for e in range(4):
             first_pass(e)
         for e in range(DIRECT):

@@ -81,16 +81,20 @@ def tile_moe_two_lin_relu_kernel(
 
         place = {}
         at = 0
-        for u in range(3):
+        head = {}
+        for j, lo, hi in ((0, 0, T), (1, 0, 1280), (1, 1280, T)):
+            head[j, lo] = keep.tile([P, hi - lo], F32, name=f"head{j}_{lo}", align_bytes=64)
+            nc.sync.dma_start(out=head[j, lo][:], in_=by_row[0][:, j, lo:hi])
+            if j == 0:
+                nc.sync.dma_start(offs_sb[:], offs)
+                nc.sync.dma_start(out=bias[:], in_=b)
+        for u in range(1, 3):
             for lo, hi in zip(PAIR_CUTS[u], PAIR_CUTS[u][1:]):
                 if (u, hi) == (2, T):
                     at = at + 8 * PIECE
                 place[u, lo] = at
                 load_pair(u, lo, hi, at)
                 at = at + 8 * (hi - lo)
-                if (u, lo) == (0, 0):
-                    nc.sync.dma_start(offs_sb[:], offs)
-                    nc.sync.dma_start(out=bias[:], in_=b)
         at = at + E * 4 * N
         place[3, 0] = at
         for lo, hi in zip(ROW_CUTS[0], ROW_CUTS[0][1:]):
@@ -112,6 +116,10 @@ def tile_moe_two_lin_relu_kernel(
             to = pairs[u][:, lo:hi].bitcast(BF16).rearrange("p (c i j) -> p c j i", i=4, j=2)
             source = raws[u, first][:, :, lo - first : hi - first].rearrange("p j (c i) -> p c j i", i=4)
             round_on(engine, to, source)
+
+        def cast_half(j, first, lo, hi, engine):
+            to = pairs[0][:, lo:hi].bitcast(BF16).rearrange("p (c j) -> p c j", j=2)[:, :, j]
+            round_on(engine, to, head[j, first][:, lo - first : hi - first])
 
         def cast_row(r, lo, hi, engine):
             first = max(c for c in ROW_CUTS[r] if c <= lo)
@@ -211,10 +219,12 @@ def tile_moe_two_lin_relu_kernel(
             )
 
         nc.scalar.activation(parked[:, (2 * (AHEAD - DIRECT) + 1) * C : 2 * (S - DIRECT * C) : 2 * C], bias[:, : E - AHEAD], COPY)
-        cast(0, 0, 480, "scalar")
-        cast(0, 480, 1280, "vector")
-        cast(0, 1280, 1568, "scalar")
-        cast(0, 1568, T, "vector")
+        for j, first in ((0, 0), (1, 0)):
+            cast_half(j, first, 0, 384, "scalar")
+            cast_half(j, first, 384, 1280, "vector")
+        for j, first in ((0, 0), (1, 1280)):
+            cast_half(j, first, 1280, 1568, "scalar")
+            cast_half(j, first, 1568, T, "vector")
         gather(0, 0, 2 * PIECE)
         gather_woven(0)
         cast(1, 0, 448, "gpsimd")

@@ -182,7 +182,7 @@ def tile_moe_two_lin_relu_kernel(
             accs[e] = psum.tile([P, C], F32, name="acc")
             nc.tensor.matmul_mx(
                 out=accs[e][:],
-                lhsT=w8_sb[:, e, :].bitcast(E4M3X4),
+                lhsT=(w8_sb[:, e, :] if e < 4 else late8[:, e - 4, :]).bitcast(E4M3X4),
                 lhsT_scale=w_planes[0][:, e, :],
                 rhs=codes0[e // 2][:, e % 2 * C : (e % 2 + 1) * C].bitcast(E4M3X4),
                 rhs_scale=planes[0][:, own],
@@ -194,7 +194,7 @@ def tile_moe_two_lin_relu_kernel(
             for h in range(0, C, 128):
                 nc.tensor.matmul_mx(
                     out=accs[e][:, h : h + 128],
-                    lhsT=w4_sb[:, e, :].bitcast(E2M1X4),
+                    lhsT=(w4_sb[:, e, :] if e < 2 else late4[:, e - 2, :]).bitcast(E2M1X4),
                     lhsT_scale=w_planes[1][:, e, :],
                     rhs=codes1[e][:, h : h + 128].bitcast(E4M3X4),
                     rhs_scale=planes[1][:, e * C + h : e * C + h + 128],
@@ -253,8 +253,10 @@ def tile_moe_two_lin_relu_kernel(
         w4_sb = reuse.tile([P, E, 2 * N], U8, name="w4_sb", offset=at, align_bytes=64)
         rows16[0] = reuse.tile([P, T], BF16, name="rows16_0", offset=at + E * 2 * N, align_bytes=64)
         w8_sb = reuse.tile([P, E, 4 * N], U8, name="w8_sb", offset=at + E * 2 * N + 2 * T, align_bytes=64)
-        nc.sync.dma_start(out=w8_sb[:].bitcast(I32), in_=w8_words.rearrange("e a p n r -> p (e a) (n r)").bitcast(I32))
-        nc.sync.dma_start(out=w4_sb[:].bitcast(I32), in_=w4_words.rearrange("e a p n -> p (e a) n").bitcast(I32))
+        w8_rows = w8_words.rearrange("e a p n r -> p (e a) (n r)")
+        w4_rows = w4_words.rearrange("e a p n -> p (e a) n")
+        nc.sync.dma_start(out=w4_sb[:, :2, :].bitcast(I32), in_=w4_rows[:, :2, :].bitcast(I32))
+        nc.sync.dma_start(out=w8_sb[:, :4, :].bitcast(I32), in_=w8_rows[:, :4, :].bitcast(I32))
         gather_third()
         woven0.append(reuse.tile([P, 2 * PIECE], U32, name="woven0_1", offset=place[2, 1280] + 64 - 8 * PIECE, align_bytes=64))
         weave(woven0[1][:], PIECE, 2 * PIECE)
@@ -263,6 +265,10 @@ def tile_moe_two_lin_relu_kernel(
         cast_row(0, 1344, T, "scalar")
         gate_sb = reuse.tile([P, S], F32, name="gate_sb", offset=place[3, 0], align_bytes=64)
         nc.sync.dma_start(out=gate_sb[:, :PIECE], in_=gate[:, :PIECE])
+        late4 = reuse.tile([P, E - 2, 2 * N], U8, name="late4", offset=place[3, 0] + 4 * S, align_bytes=64)
+        late8 = reuse.tile([P, E - 4, 4 * N], U8, name="late8", offset=place[3, 0] + 4 * S + (E - 2) * 2 * N, align_bytes=64)
+        nc.sync.dma_start(out=late4[:].bitcast(I32), in_=w4_rows[:, 2:, :].bitcast(I32))
+        nc.sync.dma_start(out=late8[:].bitcast(I32), in_=w8_rows[:, 4:, :].bitcast(I32))
         nc.sync.dma_start(out=gate_sb[:, PIECE:], in_=gate[:, PIECE:])
         for e in range(AHEAD):
             gather_row(0, e)

@@ -27,7 +27,7 @@ PIECE = 512
 PAIR_CUTS = ((0, 1280, T), (0, 768, 1536, T), (0, 1280, T))
 ROW_CUTS = ((0, 1024, T), (0, 768, 1536, T))
 AHEAD = 3
-DIRECT = 2
+DIRECT = 1
 
 
 def tile_moe_two_lin_relu_kernel(
@@ -51,12 +51,13 @@ def tile_moe_two_lin_relu_kernel(
         last0 = keep.tile([P, 2 * PIECE], U32, name="last0", align_bytes=64)
         codes1 = [keep.tile([P, C], U32, name=f"codes1_{e}", tag=f"codes1_{e}", align_bytes=64) for e in range(E)]
         planes = [keep.tile([P, S], U8, name=f"planes{a}", align_bytes=64) for a in range(2)]
-        w_planes = [keep.tile([P, E, N], U8, name="w8_planes", align_bytes=64)]
+        w_planes = [keep.tile([P, E, N], U8, name=f"w_planes{a}", align_bytes=64) for a in range(2)]
         bias = keep.tile([P, E], F32, name="bias")
         out_sb = keep.tile([P, T], F32, name="out_sb")
         acts = keep.tile([P, S], F32, name="acts")
 
-        nc.gpsimd.memset(w_planes[0][:].bitcast(I32), 0)
+        for a in range(2):
+            nc.gpsimd.memset(w_planes[a][:].bitcast(I32), 0)
         nc.vector.memset(out_sb[:], 0.0)
 
         def load_scales(q, a):
@@ -100,8 +101,23 @@ def tile_moe_two_lin_relu_kernel(
         for lo, hi in zip(ROW_CUTS[0], ROW_CUTS[0][1:]):
             load_piece(0, lo, hi, at + 4 * lo)
         nc.sync.dma_start(dst_sb[:], dst)
-        for q in range(4):
+        for q in range(2):
             load_scales(q, 0)
+        place[4, 0] = at + 4 * T
+        place[4, 1536] = place[4, 0] + 4 * 1536 + 4 * PIECE
+        load_piece(1, 0, 768, place[4, 0])
+        load_piece(1, 768, 1536, place[4, 0] + 4 * 768)
+        load_piece(1, 1536, T, place[4, 1536])
+        w8_rows = w8_words.rearrange("e a p n r -> p (e a) (n r)")
+        w4_rows = w4_words.rearrange("e a p n -> p (e a) n")
+        w4_sb = keep.tile([P, 2, 2 * N], U8, name="w4_sb", align_bytes=64)
+        w8_sb = keep.tile([P, 4, 4 * N], U8, name="w8_sb", align_bytes=64)
+        nc.sync.dma_start(out=w4_sb[:].bitcast(I32), in_=w4_rows[:, :2, :].bitcast(I32))
+        nc.sync.dma_start(out=w8_sb[:].bitcast(I32), in_=w8_rows[:, :4, :].bitcast(I32))
+        for q in range(2, 4):
+            load_scales(q, 0)
+        for q in range(4):
+            load_scales(q, 1)
 
         def round_on(engine, to, source):
             if engine == "scalar":
@@ -231,8 +247,6 @@ def tile_moe_two_lin_relu_kernel(
         cast(1, 448, 768, "scalar")
         cast(1, 768, 1088, "gpsimd")
         cast(1, 1088, 1536, "scalar")
-        load_piece(1, 0, 768, place[1, 768])
-        load_piece(1, 768, 1536, place[1, 768] + 4 * 768)
         cast(1, 1536, 1744, "scalar")
         cast(1, 1744, T, "vector")
         gather(1, 0, PIECE)
@@ -242,21 +256,10 @@ def tile_moe_two_lin_relu_kernel(
         weave(woven0[0][:], 0, PIECE)
         cast(2, 0, 640, "gpsimd")
         cast(2, 640, 1280, "scalar")
-        load_piece(1, 1536, T, place[2, 0] + 2816)
-        w_planes.append(reuse.tile([P, E, N], U8, name="w4_planes", offset=place[2, 0], align_bytes=64))
-        nc.gpsimd.memset(w_planes[1][:].bitcast(I32), 0)
-        for q in range(4):
-            load_scales(q, 1)
         cast(2, 1280, 1568, "scalar")
         cast(2, 1568, T, "vector")
         at = place[2, 1280] + 64
-        w4_sb = reuse.tile([P, E, 2 * N], U8, name="w4_sb", offset=at, align_bytes=64)
         rows16[0] = reuse.tile([P, T], BF16, name="rows16_0", offset=at + E * 2 * N, align_bytes=64)
-        w8_sb = reuse.tile([P, E, 4 * N], U8, name="w8_sb", offset=at + E * 2 * N + 2 * T, align_bytes=64)
-        w8_rows = w8_words.rearrange("e a p n r -> p (e a) (n r)")
-        w4_rows = w4_words.rearrange("e a p n -> p (e a) n")
-        nc.sync.dma_start(out=w4_sb[:, :2, :].bitcast(I32), in_=w4_rows[:, :2, :].bitcast(I32))
-        nc.sync.dma_start(out=w8_sb[:, :4, :].bitcast(I32), in_=w8_rows[:, :4, :].bitcast(I32))
         gather_third()
         woven0.append(reuse.tile([P, 2 * PIECE], U32, name="woven0_1", offset=place[2, 1280] + 64 - 8 * PIECE, align_bytes=64))
         weave(woven0[1][:], PIECE, 2 * PIECE)
@@ -277,14 +280,17 @@ def tile_moe_two_lin_relu_kernel(
         cast_row(1, 1536, T, "vector")
         for e in range(AHEAD):
             gather_row(1, e)
-        quantize0(0, woven0[0], reuse.tile([P, PIECE], U32, name="codes0_0", offset=place[2, 0] + 2816 + 64 - 4 * PIECE, align_bytes=64))
-        quantize0(1, woven0[1], reuse.tile([P, PIECE], U32, name="codes0_1", offset=place[2, 0] + 2816 + 64, align_bytes=64))
+        quantize0(0, woven0[0], reuse.tile([P, PIECE], U32, name="codes0_0", offset=place[4, 1536] + 64 - 4 * PIECE, align_bytes=64))
+        quantize0(1, woven0[1], reuse.tile([P, PIECE], U32, name="codes0_1", offset=place[4, 1536] + 64, align_bytes=64))
         for e in range(4):
             first_pass(e)
         for e in range(DIRECT):
             quantize1(e)
             second_pass(e)
         quantize0(2, last0, keep.tile([P, PIECE], U32, name="codes0_2", tag="woven0_0", align_bytes=64))
+        weave1(1, "woven1_1")
+        quantize1(1)
+        second_pass(1)
         relu(0)
         scatter(0, C)
         weave1(2, "codes1_0")

@@ -164,11 +164,15 @@ def tile_moe_two_lin_relu_kernel(
                 to = picked1[e][:, C:].bitcast(BF16).rearrange("p (s j) -> p s j", j=2)[:, :, r]
             nc.scalar.activation(to, rows16[r][:].indirect(listed(e * C, (e + 1) * C)), COPY)
 
-        def weave1(e, tag):
+        def weave1(e, tag, on_vector=False):
             woven = keep.tile([P, 2 * C], U32, name=f"woven1_{e}", tag=tag, align_bytes=64)
             woven1[e] = woven[:]
             to = woven[:].rearrange("p (c i u) -> p c u i", i=2, u=2)
-            nc.scalar.copy(to, picked1[e].rearrange("p (u c i) -> p c u i", u=2, i=2))
+            source = picked1[e].rearrange("p (u c i) -> p c u i", u=2, i=2)
+            if on_vector:
+                nc.vector.tensor_copy(out=to, in_=source)
+            else:
+                nc.scalar.copy(to, source)
 
         def weave(to, lo, hi):
             to = to.rearrange("p (c i u) -> p c u i", i=2, u=2)
@@ -287,8 +291,8 @@ def tile_moe_two_lin_relu_kernel(
         for e in range(DIRECT):
             quantize1(e)
             second_pass(e)
+        weave1(1, "woven1_1", on_vector=True)
         quantize0(2, last0, keep.tile([P, PIECE], U32, name="codes0_2", tag="woven0_0", align_bytes=64))
-        weave1(1, "woven1_1")
         quantize1(1)
         second_pass(1)
         relu(0)

@@ -101,7 +101,7 @@ def tile_moe_two_lin_relu_kernel(
         for lo, hi in zip(ROW_CUTS[0], ROW_CUTS[0][1:]):
             load_piece(0, lo, hi, at + 4 * lo)
         nc.sync.dma_start(dst_sb[:], dst)
-        for q in range(2):
+        for q in range(3):
             load_scales(q, 0)
         place[4, 0] = at + 4 * T
         place[4, 1536] = place[4, 0] + 4 * 1536 + 4 * PIECE
@@ -114,8 +114,9 @@ def tile_moe_two_lin_relu_kernel(
         w8_sb = keep.tile([P, 4, 4 * N], U8, name="w8_sb", align_bytes=64)
         nc.sync.dma_start(out=w4_sb[:].bitcast(I32), in_=w4_rows[:, :2, :].bitcast(I32))
         nc.sync.dma_start(out=w8_sb[:].bitcast(I32), in_=w8_rows[:, :4, :].bitcast(I32))
-        for q in range(2, 4):
-            load_scales(q, 0)
+        gate_first = keep.tile([P, PIECE], F32, name="gate_first", align_bytes=64)
+        nc.sync.dma_start(out=gate_first[:], in_=gate[:, :PIECE])
+        load_scales(3, 0)
         for q in range(4):
             load_scales(q, 1)
 
@@ -234,8 +235,9 @@ def tile_moe_two_lin_relu_kernel(
             nc.scalar.activation(acts[:, e * C : (e + 1) * C], accs[e][:], RELU, bias=bias_of(e))
 
         def scatter(lo, hi):
+            gates = gate_first[:, lo:hi] if hi <= PIECE else gate_rest[:, lo - PIECE : hi - PIECE]
             nc.vector.tensor_tensor(
-                out_sb[:].indirect(dst_sb[:, lo // 16 : hi // 16]), acts[:, lo:hi], gate_sb[:, lo:hi], MULT
+                out_sb[:].indirect(dst_sb[:, lo // 16 : hi // 16]), acts[:, lo:hi], gates, MULT
             )
 
         nc.scalar.activation(parked[:, (2 * (AHEAD - DIRECT) + 1) * C : 2 * (S - DIRECT * C) : 2 * C], bias[:, : E - AHEAD], COPY)
@@ -270,13 +272,12 @@ def tile_moe_two_lin_relu_kernel(
         cast_row(0, 0, 1024, "gpsimd")
         cast_row(0, 1024, 1344, "gpsimd")
         cast_row(0, 1344, T, "scalar")
-        gate_sb = reuse.tile([P, S], F32, name="gate_sb", offset=place[3, 0], align_bytes=64)
-        nc.sync.dma_start(out=gate_sb[:, :PIECE], in_=gate[:, :PIECE])
+        gate_rest = reuse.tile([P, S - PIECE], F32, name="gate_rest", offset=place[3, 0], align_bytes=64)
         late4 = reuse.tile([P, E - 2, 2 * N], U8, name="late4", offset=place[3, 0] + 4 * S, align_bytes=64)
         late8 = reuse.tile([P, E - 4, 4 * N], U8, name="late8", offset=place[3, 0] + 4 * S + (E - 2) * 2 * N, align_bytes=64)
         nc.sync.dma_start(out=late4[:].bitcast(I32), in_=w4_rows[:, 2:, :].bitcast(I32))
         nc.sync.dma_start(out=late8[:].bitcast(I32), in_=w8_rows[:, 4:, :].bitcast(I32))
-        nc.sync.dma_start(out=gate_sb[:, PIECE:], in_=gate[:, PIECE:])
+        nc.sync.dma_start(out=gate_rest[:], in_=gate[:, PIECE:])
         for e in range(AHEAD):
             gather_row(0, e)
         cast_row(1, 0, 768, "gpsimd")

@@ -17,17 +17,18 @@ COPY = mybir.ActivationFunctionType.Copy
 RELU = mybir.ActivationFunctionType.Relu
 MULT = mybir.AluOpType.mult
 ADD = mybir.AluOpType.add
+MAX = mybir.AluOpType.max
 
 FLOPS = 2 * K * N * S
 
 P = 128
 PACK = 4
 K_PASS = P * PACK
-PIECE = 512
-PAIR_CUTS = ((0, 1280, T), (0, 768, 1536, T), (0, 1280, T))
-ROW_CUTS = ((0, 1024, T), (0, 768, 1536, T))
-AHEAD = 3
-DIRECT = 1
+PIECE = 2 * C
+PAIR_CUTS = ((0, 1280, T), (0, 1536, T))
+SCALAR_SHARE = {(0, 1280): 256, (1, 0): 768}
+EARLY = 2
+STORE = 512
 
 
 def tile_moe_two_lin_relu_kernel(
@@ -36,283 +37,248 @@ def tile_moe_two_lin_relu_kernel(
     nc = tc.nc
     with ExitStack() as ctx:
         keep = ctx.enter_context(tc.tile_pool(name="keep", bufs=1))
-        reuse = ctx.enter_context(tc.tile_pool(name="reuse", bufs=1))
-        psum = ctx.enter_context(tc.psum_pool(name="psum", bufs=4))
+        psum = ctx.enter_context(tc.psum_pool(name="psum", bufs=E))
+
+        def tile(shape, dtype, name, tag=None):
+            return keep.tile(shape, dtype, name=name, tag=tag or name, align_bytes=64)
 
         offs_sb = keep.tile([P, S // 16], U16, name="offs_sb")
         dst_sb = keep.tile([P, S // 16], U16, name="dst_sb")
-        pairs = [keep.tile([P, T], U32, name=f"pairs{u}", align_bytes=64) for u in range(3)]
-        rows16 = {1: keep.tile([P, T], BF16, name="rows16_1", align_bytes=64)}
-        picked = keep.tile([P, 2, 2 * PIECE], U32, name="picked", align_bytes=64)
-        first1 = keep.tile([P, 2 * DIRECT * C], U32, name="first1", align_bytes=64)
-        rest1 = keep.tile([P, 2 * (S - DIRECT * C)], U32, name="rest1", align_bytes=64)
-        picked1 = {e: rest1[:, 2 * (e - DIRECT) * C : 2 * (e - DIRECT + 1) * C] for e in range(DIRECT, E)}
-        woven1 = {e: first1[:, 2 * e * C : 2 * (e + 1) * C] for e in range(DIRECT)}
-        last0 = keep.tile([P, 2 * PIECE], U32, name="last0", align_bytes=64)
-        codes1 = [keep.tile([P, C], U32, name=f"codes1_{e}", tag=f"codes1_{e}", align_bytes=64) for e in range(E)]
-        planes = [keep.tile([P, S], U8, name=f"planes{a}", align_bytes=64) for a in range(2)]
-        w_planes = [keep.tile([P, E, N], U8, name=f"w_planes{a}", align_bytes=64) for a in range(2)]
-        bias = keep.tile([P, E], F32, name="bias")
-        out_sb = keep.tile([P, T], F32, name="out_sb")
-        acts = keep.tile([P, S], F32, name="acts")
-
+        w_planes = [tile([P, E, N], U8, f"w_planes{a}") for a in range(2)]
+        windows = [tile([P, T], F32, f"window{i}") for i in range(2)]
         for a in range(2):
             nc.gpsimd.memset(w_planes[a][:].bitcast(I32), 0)
-        nc.vector.memset(out_sb[:], 0.0)
 
-        def load_scales(q, a):
+        nc.vector.memset(windows[0][:], 0.0)
+        nc.scalar.activation(windows[1][:], windows[0][:], COPY)
+
+        by_row = [xT[a * K_PASS : (a + 1) * K_PASS, :].rearrange("(p j) w -> p j w", j=PACK) for a in range(2)]
+        rows = {}
+        raws = {}
+
+        def load_row(a, j):
+            rows[a, j] = tile([P, T], F32, f"row{a}_{j}")
+            nc.sync.dma_start(out=rows[a, j][:], in_=by_row[a][:, j, :])
+
+        def load_pair(a, i):
+            lo, hi = PAIR_CUTS[a][i : i + 2]
+            raws[a, lo] = tile([P, 2, hi - lo], F32, f"raw{a}_{lo}")
+            nc.sync.dma_start(out=raws[a, lo][:], in_=by_row[a][:, 0:2, lo:hi])
+
+        def load_scales(a, q):
             scales = (w8_scales, w4_scales)[a]
             nc.sync.dma_start(
                 out=w_planes[a][32 * q : 32 * q + 4].bitcast(I32),
                 in_=scales[:, :, 4 * q : 4 * q + 4, :].rearrange("e a q n -> q (e a) n").bitcast(I32),
             )
 
-        by_row = [xT[a * K_PASS : (a + 1) * K_PASS, :].rearrange("(p j) w -> p j w", j=PACK) for a in range(2)]
-        raws = {}
+        w_rows = (w8_words.rearrange("e a p n r -> p (e a) (n r)"), w4_words.rearrange("e a p n -> p (e a) n"))
+        w_sb = {}
 
-        def load_pair(u, lo, hi, at):
-            raw = reuse.tile([P, 2, hi - lo], F32, name=f"raw{u}_{lo}", offset=at, align_bytes=64)
-            nc.sync.dma_start(out=raw[:], in_=by_row[u // 2][:, 2 * (u % 2) : 2 * (u % 2) + 2, lo:hi])
-            raws[u, lo] = raw
+        def load_weights(a, lo, hi):
+            part = tile([P, hi - lo, w_rows[a].shape[2]], U8, f"w{a}_{lo}")
+            nc.sync.dma_start(out=part[:].bitcast(I32), in_=w_rows[a][:, lo:hi, :].bitcast(I32))
+            for e in range(lo, hi):
+                w_sb[a, e] = part[:, e - lo, :]
 
-        def load_piece(r, lo, hi, at):
-            raw = reuse.tile([P, hi - lo], F32, name=f"row{r}_{lo}", offset=at, align_bytes=64)
-            nc.sync.dma_start(out=raw[:], in_=by_row[1][:, 2 + r, lo:hi])
-            raws[3 + r, lo] = raw
+        gates = {}
 
-        place = {}
-        at = 0
-        head = {}
-        for j, lo, hi in ((0, 0, T), (1, 0, 1280), (1, 1280, T)):
-            head[j, lo] = keep.tile([P, hi - lo], F32, name=f"head{j}_{lo}", align_bytes=64)
-            nc.sync.dma_start(out=head[j, lo][:], in_=by_row[0][:, j, lo:hi])
-            if j == 0:
-                nc.sync.dma_start(offs_sb[:], offs)
-                nc.sync.dma_start(out=bias[:], in_=b)
-        for u in range(1, 3):
-            for lo, hi in zip(PAIR_CUTS[u], PAIR_CUTS[u][1:]):
-                if (u, hi) == (2, T):
-                    at = at + 8 * PIECE
-                place[u, lo] = at
-                load_pair(u, lo, hi, at)
-                at = at + 8 * (hi - lo)
-        at = at + E * 4 * N
-        place[3, 0] = at
-        for lo, hi in zip(ROW_CUTS[0], ROW_CUTS[0][1:]):
-            load_piece(0, lo, hi, at + 4 * lo)
+        def load_gate(lo, hi):
+            part = tile([P, (hi - lo) * C], F32, f"gate{lo}")
+            nc.sync.dma_start(out=part[:], in_=gate[:, lo * C : hi * C])
+            for e in range(lo, hi):
+                gates[e] = (part, lo)
+
+        def gate_of(lo, hi):
+            part, first = gates[lo]
+            return part[:, (lo - first) * C : (hi - first) * C]
+
+        bias = tile([P, E], F32, "bias")
+
+        load_row(0, 2)
+        nc.sync.dma_start(offs_sb[:], offs)
+        nc.sync.dma_start(out=bias[:], in_=b)
+        load_pair(0, 0)
+        load_pair(0, 1)
+        load_scales(0, 0)
+        load_scales(0, 1)
+        load_row(0, 3)
+        load_scales(0, 2)
+        load_scales(0, 3)
+        load_pair(1, 0)
         nc.sync.dma_start(dst_sb[:], dst)
-        for q in range(3):
-            load_scales(q, 0)
-        place[4, 0] = at + 4 * T
-        place[4, 1536] = place[4, 0] + 4 * 1536 + 4 * PIECE
-        load_piece(1, 0, 768, place[4, 0])
-        load_piece(1, 768, 1536, place[4, 0] + 4 * 768)
-        load_piece(1, 1536, T, place[4, 1536])
-        w8_rows = w8_words.rearrange("e a p n r -> p (e a) (n r)")
-        w4_rows = w4_words.rearrange("e a p n -> p (e a) n")
-        w4_sb = keep.tile([P, 2, 2 * N], U8, name="w4_sb", align_bytes=64)
-        w8_sb = keep.tile([P, 4, 4 * N], U8, name="w8_sb", align_bytes=64)
-        nc.sync.dma_start(out=w4_sb[:].bitcast(I32), in_=w4_rows[:, :2, :].bitcast(I32))
-        nc.sync.dma_start(out=w8_sb[:].bitcast(I32), in_=w8_rows[:, :4, :].bitcast(I32))
-        gate_first = keep.tile([P, PIECE], F32, name="gate_first", align_bytes=64)
-        nc.sync.dma_start(out=gate_first[:], in_=gate[:, :PIECE])
-        load_scales(3, 0)
+        load_pair(1, 1)
+        load_row(1, 2)
+        load_row(1, 3)
+        load_weights(0, 0, EARLY)
+        load_weights(1, 0, EARLY)
+        load_gate(0, EARLY)
         for q in range(4):
-            load_scales(q, 1)
+            load_scales(1, q)
+        load_weights(1, EARLY, E)
+        load_weights(0, EARLY, E)
+        load_gate(EARLY, E)
 
-        def round_on(engine, to, source):
-            if engine == "scalar":
-                nc.scalar.activation(to, source, COPY)
-            elif engine == "gpsimd":
-                nc.gpsimd.tensor_scalar(to, source, 1.0, 0.0, MULT, ADD)
-            else:
-                nc.vector.tensor_copy(out=to, in_=source)
-
-        def cast(u, lo, hi, engine):
-            first = max(c for c in PAIR_CUTS[u] if c <= lo)
-            to = pairs[u][:, lo:hi].bitcast(BF16).rearrange("p (c i j) -> p c j i", i=4, j=2)
-            source = raws[u, first][:, :, lo - first : hi - first].rearrange("p j (c i) -> p c j i", i=4)
-            round_on(engine, to, source)
-
-        def cast_half(j, first, lo, hi, engine):
-            to = pairs[0][:, lo:hi].bitcast(BF16).rearrange("p (c j) -> p c j", j=2)[:, :, j]
-            round_on(engine, to, head[j, first][:, lo - first : hi - first])
-
-        def cast_row(r, lo, hi, engine):
-            first = max(c for c in ROW_CUTS[r] if c <= lo)
-            round_on(engine, rows16[r][:, lo:hi], raws[3 + r, first][:, lo - first : hi - first])
+        pairs = [tile([P, T], U32, f"pairs{a}") for a in range(2)]
+        both = tile([P, 4 * S], U32, "picked")
+        picked = [both[:, 2 * S * a : 2 * S * (a + 1)] for a in range(2)]
+        planes = [tile([P, S], U8, f"planes{a}") for a in range(2)]
+        acts = tile([P, S], F32, "acts")
 
         def listed(lo, hi):
             return offs_sb[:, lo // 16 : hi // 16]
 
-        def gather(u, lo, hi):
-            nc.vector.tensor_copy(picked[:, u, lo:hi], pairs[u][:].indirect(listed(lo, hi)))
+        def round_pair(a, i):
+            first, last = PAIR_CUTS[a][i : i + 2]
+            cut = first + SCALAR_SHARE.get((a, first), 0)
+            for lo, hi in ((first, cut), (cut, last)):
+                if lo == hi:
+                    continue
+                to = pairs[a][:, lo:hi].bitcast(BF16).rearrange("p (c i j) -> p c j i", i=4, j=2)
+                source = raws[a, first][:, :, lo - first : hi - first].rearrange("p j (c i) -> p c j i", i=4)
+                if hi == cut:
+                    nc.scalar.activation(to, source, COPY)
+                else:
+                    nc.vector.tensor_copy(out=to, in_=source)
 
-        def gather_woven(u):
-            to = last0[:].rearrange("p (s u) -> p s u", u=2)[:, :, u]
-            nc.vector.tensor_copy(to, pairs[u][:].indirect(listed(2 * PIECE, S)))
+        def gather_pair(a):
+            nc.vector.tensor_copy(picked[a][:, :S], pairs[a][:].indirect(offs_sb[:]))
 
-        def gather_third():
-            to = first1[:].rearrange("p (s u) -> p s u", u=2)[:, :, 0]
-            nc.vector.tensor_copy(to, pairs[2][:].indirect(listed(0, DIRECT * C)))
-            to = rest1[:].rearrange("p (e u c) -> p e u c", u=2, c=C)[:, :, 0, :]
-            nc.vector.tensor_copy(to, pairs[2][:].indirect(listed(DIRECT * C, S)))
+        def gather_row(a, j, lo, hi):
+            to = picked[a][:, S + lo : S + hi].bitcast(BF16).rearrange("p (s h) -> p s h", h=2)[:, :, j - 2]
+            nc.scalar.activation(to, rows[a, j][:].indirect(listed(lo, hi)), COPY)
 
-        def gather_row(r, e):
-            if e < DIRECT:
-                to = woven1[e].bitcast(BF16).rearrange("p (s j) -> p s j", j=PACK)[:, :, 2 + r]
-            else:
-                to = picked1[e][:, C:].bitcast(BF16).rearrange("p (s j) -> p s j", j=2)[:, :, r]
-            nc.scalar.activation(to, rows16[r][:].indirect(listed(e * C, (e + 1) * C)), COPY)
-
-        def weave1(e, tag, on_vector=False):
-            woven = keep.tile([P, 2 * C], U32, name=f"woven1_{e}", tag=tag, align_bytes=64)
-            woven1[e] = woven[:]
-            to = woven[:].rearrange("p (c i u) -> p c u i", i=2, u=2)
-            source = picked1[e].rearrange("p (u c i) -> p c u i", u=2, i=2)
-            if on_vector:
-                nc.vector.tensor_copy(out=to, in_=source)
-            else:
+        def weave(a, lo, hi, woven, on_scalar=False):
+            to = woven.rearrange("p (c i u) -> p c u i", i=2, u=2)
+            source = picked[a].rearrange("p (u s) -> p u s", u=2)[:, :, lo:hi].rearrange("p u (c i) -> p c u i", i=2)
+            if on_scalar:
                 nc.scalar.copy(to, source)
+            else:
+                nc.vector.tensor_copy(out=to, in_=source)
 
-        def weave(to, lo, hi):
-            to = to.rearrange("p (c i u) -> p c u i", i=2, u=2)
-            nc.scalar.copy(to, picked[:, :, lo:hi].rearrange("p u (c i) -> p c u i", i=2))
+        codes = {}
 
-        codes0 = {}
-
-        def quantize0(i, woven, codes):
-            codes0[i] = codes
-            nc.vector.quantize_mx(
-                out=codes0[i][:].bitcast(E4M3X4),
-                scales=planes[0][:, i * PIECE : (i + 1) * PIECE],
-                in_=woven[:].bitcast(BF16),
-            )
-
-        def quantize1(e):
-            nc.vector.quantize_mx(
-                out=codes1[e][:].bitcast(E4M3X4),
-                scales=planes[1][:, e * C : (e + 1) * C],
-                in_=woven1[e].bitcast(BF16),
-            )
+        def quantize(a, lo, hi, woven):
+            made = tile([P, hi - lo], U32, f"codes{a}_{lo}")
+            nc.vector.quantize_mx(out=made[:].bitcast(E4M3X4), scales=planes[a][:, lo:hi], in_=woven.bitcast(BF16))
+            for e in range(lo // C, hi // C):
+                codes[a, e] = made[:, e * C - lo : (e + 1) * C - lo]
 
         accs = {}
 
-        def first_pass(e):
-            own = slice(e * C, (e + 1) * C)
-            accs[e] = psum.tile([P, C], F32, name="acc")
+        def product(a, e):
+            first = e not in accs
+            if first:
+                accs[e] = psum.tile([P, C], F32, name="acc")
             nc.tensor.matmul_mx(
                 out=accs[e][:],
-                lhsT=(w8_sb[:, e, :] if e < 4 else late8[:, e - 4, :]).bitcast(E4M3X4),
-                lhsT_scale=w_planes[0][:, e, :],
-                rhs=codes0[e // 2][:, e % 2 * C : (e % 2 + 1) * C].bitcast(E4M3X4),
-                rhs_scale=planes[0][:, own],
-                start=True,
-                stop=False,
+                lhsT=w_sb[a, e].bitcast((E4M3X4, E2M1X4)[a]),
+                lhsT_scale=w_planes[a][:, e, :],
+                rhs=codes[a, e].bitcast(E4M3X4),
+                rhs_scale=planes[a][:, e * C : (e + 1) * C],
+                start=first,
+                stop=not first,
             )
 
-        def second_pass(e):
-            for h in range(0, C, 128):
-                nc.tensor.matmul_mx(
-                    out=accs[e][:, h : h + 128],
-                    lhsT=(w4_sb[:, e, :] if e < 2 else late4[:, e - 2, :]).bitcast(E2M1X4),
-                    lhsT_scale=w_planes[1][:, e, :],
-                    rhs=codes1[e][:, h : h + 128].bitcast(E4M3X4),
-                    rhs_scale=planes[1][:, e * C + h : e * C + h + 128],
-                    start=False,
-                    stop=(h + 128 == C),
-                )
+        def relu(e, on_vector=False):
+            to = acts[:, e * C : (e + 1) * C]
+            if on_vector:
+                nc.vector.tensor_scalar(to, accs[e][:], bias[:, e : e + 1], 0.0, ADD, MAX)
+            else:
+                nc.scalar.activation(to, accs[e][:], RELU, bias=bias[:, e : e + 1])
 
-        parked = rest1[:].bitcast(F32)
+        def places(lo, hi):
+            return dst_sb[:, lo * C // 16 : hi * C // 16]
 
-        def bias_of(e):
-            if e + AHEAD < E:
-                at = (2 * (e + AHEAD - DIRECT) + 1) * C
-                return parked[:, at : at + 1]
-            return bias[:, e : e + 1]
+        def scatter_gating(lo, hi):
+            nc.vector.tensor_tensor(windows[0][:].indirect(places(lo, hi)), acts[:, lo * C : hi * C], gate_of(lo, hi), MULT)
 
-        def relu(e):
-            nc.scalar.activation(acts[:, e * C : (e + 1) * C], accs[e][:], RELU, bias=bias_of(e))
+        gated = {}
 
-        def scatter(lo, hi):
-            gates = gate_first[:, lo:hi] if hi <= PIECE else gate_rest[:, lo - PIECE : hi - PIECE]
-            nc.vector.tensor_tensor(
-                out_sb[:].indirect(dst_sb[:, lo // 16 : hi // 16]), acts[:, lo:hi], gates, MULT
-            )
+        def apply_gate(lo, hi, tag):
+            made = tile([P, (hi - lo) * C], F32, f"gated{lo}", tag)
+            nc.vector.tensor_tensor(made[:], acts[:, lo * C : hi * C], gate_of(lo, hi), MULT)
+            for e in range(lo, hi):
+                gated[e] = made[:, (e - lo) * C : (e - lo + 1) * C]
 
-        nc.scalar.activation(parked[:, (2 * (AHEAD - DIRECT) + 1) * C : 2 * (S - DIRECT * C) : 2 * C], bias[:, : E - AHEAD], COPY)
-        for j, first in ((0, 0), (1, 0)):
-            cast_half(j, first, 0, 384, "scalar")
-            cast_half(j, first, 384, 1280, "vector")
-        for j, first in ((0, 0), (1, 1280)):
-            cast_half(j, first, 1280, 1568, "scalar")
-            cast_half(j, first, 1568, T, "vector")
-        gather(0, 0, 2 * PIECE)
-        gather_woven(0)
-        cast(1, 0, 448, "gpsimd")
-        cast(1, 448, 768, "scalar")
-        cast(1, 768, 1088, "gpsimd")
-        cast(1, 1088, 1536, "scalar")
-        cast(1, 1536, 1744, "scalar")
-        cast(1, 1744, T, "vector")
-        gather(1, 0, PIECE)
-        gather(1, PIECE, 2 * PIECE)
-        gather_woven(1)
-        woven0 = [keep.tile([P, 2 * PIECE], U32, name="woven0_0", tag="woven0_0", align_bytes=64)]
-        weave(woven0[0][:], 0, PIECE)
-        cast(2, 0, 640, "gpsimd")
-        cast(2, 640, 1280, "scalar")
-        cast(2, 1280, 1568, "scalar")
-        cast(2, 1568, T, "vector")
-        at = place[2, 1280] + 64
-        rows16[0] = reuse.tile([P, T], BF16, name="rows16_0", offset=at + E * 2 * N, align_bytes=64)
-        gather_third()
-        woven0.append(reuse.tile([P, 2 * PIECE], U32, name="woven0_1", offset=place[2, 1280] + 64 - 8 * PIECE, align_bytes=64))
-        weave(woven0[1][:], PIECE, 2 * PIECE)
-        cast_row(0, 0, 1024, "gpsimd")
-        cast_row(0, 1024, 1344, "gpsimd")
-        cast_row(0, 1344, T, "scalar")
-        gate_rest = reuse.tile([P, S - PIECE], F32, name="gate_rest", offset=place[3, 0], align_bytes=64)
-        late4 = reuse.tile([P, E - 2, 2 * N], U8, name="late4", offset=place[3, 0] + 4 * S, align_bytes=64)
-        late8 = reuse.tile([P, E - 4, 4 * N], U8, name="late8", offset=place[3, 0] + 4 * S + (E - 2) * 2 * N, align_bytes=64)
-        nc.sync.dma_start(out=late4[:].bitcast(I32), in_=w4_rows[:, 2:, :].bitcast(I32))
-        nc.sync.dma_start(out=late8[:].bitcast(I32), in_=w8_rows[:, 4:, :].bitcast(I32))
-        nc.sync.dma_start(out=gate_rest[:], in_=gate[:, PIECE:])
-        for e in range(AHEAD):
-            gather_row(0, e)
-        cast_row(1, 0, 768, "gpsimd")
-        cast_row(1, 768, 1536, "gpsimd")
-        cast_row(1, 1536, T, "vector")
-        for e in range(AHEAD):
-            gather_row(1, e)
-        quantize0(0, woven0[0], reuse.tile([P, PIECE], U32, name="codes0_0", offset=place[4, 1536] + 64 - 4 * PIECE, align_bytes=64))
-        quantize0(1, woven0[1], reuse.tile([P, PIECE], U32, name="codes0_1", offset=place[4, 1536] + 64, align_bytes=64))
+        def scatter_gated(e):
+            nc.scalar.activation(windows[1][:].indirect(places(e, e + 1)), gated[e], COPY)
+
+        gather_row(0, 2, 0, S // 2)
+        gather_row(0, 2, S // 2, S)
+        round_pair(0, 0)
+        round_pair(0, 1)
+        gather_pair(0)
+        for i in range(3):
+            gather_row(0, 3, i * PIECE, (i + 1) * PIECE)
+        woven0 = [tile([P, 2 * PIECE], U32, f"woven0_{i}") for i in range(2)]
+        for i in range(2):
+            weave(0, i * PIECE, (i + 1) * PIECE, woven0[i][:])
+        for i in range(2):
+            quantize(0, i * PIECE, (i + 1) * PIECE, woven0[i][:])
+        round_pair(1, 0)
+        woven0.append(tile([P, 2 * PIECE], U32, "woven0_2", "raw1_0"))
+        weave(0, 2 * PIECE, S, woven0[2][:], on_scalar=True)
+        round_pair(1, 1)
+        gather_pair(1)
+        quantize(0, 2 * PIECE, S, woven0[2][:])
+
+        gather_row(1, 2, 0, PIECE)
+        gather_row(1, 2, PIECE, 2 * PIECE)
+        for e in range(EARLY):
+            product(0, e)
+        woven1 = {1: picked[1][:, S + 2 * PIECE :]}
+
+        def weave1(e, tag=None):
+            if e not in woven1:
+                woven1[e] = tile([P, 2 * C], U32, f"woven1_{e}", tag)[:]
+            weave(1, e * C, (e + 1) * C, woven1[e])
+
+        def finish(e):
+            quantize(1, e * C, (e + 1) * C, woven1[e])
+
+        def multiply(e):
+            product(1, e)
+            if e >= EARLY:
+                product(0, e)
+
         for e in range(4):
-            first_pass(e)
-        for e in range(DIRECT):
-            quantize1(e)
-            second_pass(e)
-        weave1(1, "woven1_1", on_vector=True)
-        quantize0(2, last0, keep.tile([P, PIECE], U32, name="codes0_2", tag="woven0_0", align_bytes=64))
-        quantize1(1)
-        second_pass(1)
-        relu(0)
-        scatter(0, C)
-        weave1(2, "codes1_0")
-        quantize1(2)
-        second_pass(2)
-        for e in range(AHEAD, E):
-            gather_row(0, e)
-            gather_row(1, e)
-            relu(e - 2)
-            scatter((e - 2) * C, (e - 1) * C)
-            weave1(e, f"woven1_{e}")
-            quantize1(e)
-            if e >= 4:
-                first_pass(e)
-            second_pass(e)
-        for e in (E - 2, E - 1):
-            relu(e)
-            scatter(e * C, (e + 1) * C)
-        nc.sync.dma_start(out=out[:, : T // 2], in_=out_sb[:, : T // 2])
-        nc.scalar.dma_start(out=out[:, T // 2 :], in_=out_sb[:, T // 2 :])
+            gather_row(1, 3, e * C, (e + 1) * C)
+        weave1(0)
+        weave1(1)
+        finish(0)
+        multiply(0)
+        finish(1)
+        multiply(1)
+        gather_row(1, 2, 2 * PIECE, S)
+        gather_row(1, 3, 4 * C, 5 * C)
+        gather_row(1, 3, 5 * C, 6 * C)
+        weave1(2)
+        weave1(3)
+        finish(2)
+        multiply(2)
+        finish(3)
+        multiply(3)
+        relu(0, on_vector=True)
+        relu(1)
+        relu(2)
+        relu(3)
+        weave1(4, "codes1_0")
+        apply_gate(0, 1, None)
+        scatter_gated(0)
+        weave1(5, f"codes1_{C}")
+        finish(4)
+        multiply(4)
+        finish(5)
+        multiply(5)
+        relu(4)
+        relu(5)
+        scatter_gating(1, 2)
+        apply_gate(2, 4, f"codes1_{5 * C}")
+        scatter_gated(2)
+        scatter_gated(3)
+        scatter_gating(4, 6)
+        for i, lo in enumerate(range(0, T, STORE)):
+            total = tile([P, STORE], F32, f"total{i}")
+            nc.vector.tensor_tensor(total[:], windows[0][:, lo : lo + STORE], windows[1][:, lo : lo + STORE], ADD)
+            (nc.sync, nc.scalar)[i % 2].dma_start(out=out[:, lo : lo + STORE], in_=total[:])

@@ -17,7 +17,6 @@ COPY = mybir.ActivationFunctionType.Copy
 RELU = mybir.ActivationFunctionType.Relu
 MULT = mybir.AluOpType.mult
 ADD = mybir.AluOpType.add
-MAX = mybir.AluOpType.max
 
 FLOPS = 2 * K * N * S
 
@@ -25,9 +24,9 @@ P = 128
 PACK = 4
 K_PASS = P * PACK
 PIECE = 2 * C
-PAIR_CUTS = ((0, 1280, T), (0, 1536, T))
-SCALAR_SHARE = {(0, 1280): 256, (1, 0): 768}
-EARLY = 2
+VECTOR_FROM = (768, 768, 928)
+SHARED = 3 * C
+SCATTER = SHARED // 2
 STORE = 512
 
 
@@ -49,21 +48,17 @@ def tile_moe_two_lin_relu_kernel(
         for a in range(2):
             nc.gpsimd.memset(w_planes[a][:].bitcast(I32), 0)
 
-        nc.vector.memset(windows[0][:], 0.0)
-        nc.scalar.activation(windows[1][:], windows[0][:], COPY)
+        nc.vector.memset(windows[0][:, : T // 2], 0.0)
+        nc.scalar.activation(windows[1][:, : T // 2], windows[0][:, : T // 2], COPY)
+        for window in windows:
+            nc.vector.memset(window[:, T // 2 :], 0.0)
 
         by_row = [xT[a * K_PASS : (a + 1) * K_PASS, :].rearrange("(p j) w -> p j w", j=PACK) for a in range(2)]
         rows = {}
-        raws = {}
 
         def load_row(a, j):
             rows[a, j] = tile([P, T], F32, f"row{a}_{j}")
             nc.sync.dma_start(out=rows[a, j][:], in_=by_row[a][:, j, :])
-
-        def load_pair(a, i):
-            lo, hi = PAIR_CUTS[a][i : i + 2]
-            raws[a, lo] = tile([P, 2, hi - lo], F32, f"raw{a}_{lo}")
-            nc.sync.dma_start(out=raws[a, lo][:], in_=by_row[a][:, 0:2, lo:hi])
 
         def load_scales(a, q):
             scales = (w8_scales, w4_scales)[a]
@@ -75,51 +70,36 @@ def tile_moe_two_lin_relu_kernel(
         w_rows = (w8_words.rearrange("e a p n r -> p (e a) (n r)"), w4_words.rearrange("e a p n -> p (e a) n"))
         w_sb = {}
 
-        def load_weights(a, lo, hi):
-            part = tile([P, hi - lo, w_rows[a].shape[2]], U8, f"w{a}_{lo}")
-            nc.sync.dma_start(out=part[:].bitcast(I32), in_=w_rows[a][:, lo:hi, :].bitcast(I32))
-            for e in range(lo, hi):
-                w_sb[a, e] = part[:, e - lo, :]
-
-        gates = {}
-
-        def load_gate(lo, hi):
-            part = tile([P, (hi - lo) * C], F32, f"gate{lo}")
-            nc.sync.dma_start(out=part[:], in_=gate[:, lo * C : hi * C])
-            for e in range(lo, hi):
-                gates[e] = (part, lo)
-
-        def gate_of(lo, hi):
-            part, first = gates[lo]
-            return part[:, (lo - first) * C : (hi - first) * C]
+        def load_weights(a):
+            part = tile([P, E, w_rows[a].shape[2]], U8, f"w{a}")
+            nc.sync.dma_start(out=part[:].bitcast(I32), in_=w_rows[a].bitcast(I32))
+            for e in range(E):
+                w_sb[a, e] = part[:, e, :]
 
         bias = tile([P, E], F32, "bias")
 
-        load_row(0, 2)
+        load_row(0, 0)
         nc.sync.dma_start(offs_sb[:], offs)
         nc.sync.dma_start(out=bias[:], in_=b)
-        load_pair(0, 0)
-        load_pair(0, 1)
+        load_row(0, 1)
+        load_row(0, 2)
         load_scales(0, 0)
         load_scales(0, 1)
         load_row(0, 3)
         load_scales(0, 2)
         load_scales(0, 3)
-        load_pair(1, 0)
+        load_row(1, 0)
         nc.sync.dma_start(dst_sb[:], dst)
-        load_pair(1, 1)
-        load_row(1, 2)
-        load_row(1, 3)
-        load_weights(0, 0, EARLY)
-        load_weights(1, 0, EARLY)
-        load_gate(0, EARLY)
+        for j in range(1, PACK):
+            load_row(1, j)
+        load_weights(0)
+        load_weights(1)
         for q in range(4):
             load_scales(1, q)
-        load_weights(1, EARLY, E)
-        load_weights(0, EARLY, E)
-        load_gate(EARLY, E)
+        gates = [tile([P, hi - lo], F32, f"gate{lo}") for lo, hi in ((0, SHARED), (SHARED, S))]
+        nc.sync.dma_start(out=gates[0][:], in_=gate[:, :SHARED])
+        nc.sync.dma_start(out=gates[1][:], in_=gate[:, SHARED:])
 
-        pairs = [tile([P, T], U32, f"pairs{a}") for a in range(2)]
         both = tile([P, 4 * S], U32, "picked")
         picked = [both[:, 2 * S * a : 2 * S * (a + 1)] for a in range(2)]
         planes = [tile([P, S], U8, f"planes{a}") for a in range(2)]
@@ -128,33 +108,20 @@ def tile_moe_two_lin_relu_kernel(
         def listed(lo, hi):
             return offs_sb[:, lo // 16 : hi // 16]
 
-        def round_pair(a, i):
-            first, last = PAIR_CUTS[a][i : i + 2]
-            cut = first + SCALAR_SHARE.get((a, first), 0)
-            for lo, hi in ((first, cut), (cut, last)):
-                if lo == hi:
-                    continue
-                to = pairs[a][:, lo:hi].bitcast(BF16).rearrange("p (c i j) -> p c j i", i=4, j=2)
-                source = raws[a, first][:, :, lo - first : hi - first].rearrange("p j (c i) -> p c j i", i=4)
-                if hi == cut:
-                    nc.scalar.activation(to, source, COPY)
-                else:
-                    nc.vector.tensor_copy(out=to, in_=source)
-
-        def gather_pair(a):
-            nc.vector.tensor_copy(picked[a][:, :S], pairs[a][:].indirect(offs_sb[:]))
-
-        def gather_row(a, j, lo, hi):
-            to = picked[a][:, S + lo : S + hi].bitcast(BF16).rearrange("p (s h) -> p s h", h=2)[:, :, j - 2]
-            nc.scalar.activation(to, rows[a, j][:].indirect(listed(lo, hi)), COPY)
-
-        def weave(a, lo, hi, woven, on_scalar=False):
-            to = woven.rearrange("p (c i u) -> p c u i", i=2, u=2)
-            source = picked[a].rearrange("p (u s) -> p u s", u=2)[:, :, lo:hi].rearrange("p u (c i) -> p c u i", i=2)
-            if on_scalar:
-                nc.scalar.copy(to, source)
+        def gather_row(a, j, lo, hi, on_vector=False):
+            half = S * (j // 2)
+            to = picked[a][:, half + lo : half + hi].bitcast(BF16).rearrange("p (s h) -> p s h", h=2)[:, :, j % 2]
+            if on_vector:
+                nc.vector.tensor_copy(to, rows[a, j][:].indirect(listed(lo, hi)))
             else:
-                nc.vector.tensor_copy(out=to, in_=source)
+                nc.scalar.activation(to, rows[a, j][:].indirect(listed(lo, hi)), COPY)
+
+        def weave(a, lo, hi):
+            woven = tile([P, 2 * (hi - lo)], U32, f"woven{a}_{lo}")
+            to = woven[:].rearrange("p (c i u) -> p c u i", i=2, u=2)
+            source = picked[a].rearrange("p (u s) -> p u s", u=2)[:, :, lo:hi].rearrange("p u (c i) -> p c u i", i=2)
+            nc.vector.tensor_copy(out=to, in_=source)
+            return woven[:]
 
         codes = {}
 
@@ -180,104 +147,45 @@ def tile_moe_two_lin_relu_kernel(
                 stop=not first,
             )
 
-        def relu(e, on_vector=False):
-            to = acts[:, e * C : (e + 1) * C]
-            if on_vector:
-                nc.vector.tensor_scalar(to, accs[e][:], bias[:, e : e + 1], 0.0, ADD, MAX)
-            else:
-                nc.scalar.activation(to, accs[e][:], RELU, bias=bias[:, e : e + 1])
+        def relu(e):
+            nc.scalar.activation(acts[:, e * C : (e + 1) * C], accs[e][:], RELU, bias=bias[:, e : e + 1])
 
         def places(lo, hi):
-            return dst_sb[:, lo * C // 16 : hi * C // 16]
+            return dst_sb[:, lo // 16 : hi // 16]
 
-        def scatter_gating(lo, hi):
-            nc.vector.tensor_tensor(windows[0][:].indirect(places(lo, hi)), acts[:, lo * C : hi * C], gate_of(lo, hi), MULT)
+        def gather_shared(r):
+            a, j = divmod(r, PACK)
+            gather_row(a, j, 0, VECTOR_FROM[r // 2])
+            gather_row(a, j, VECTOR_FROM[r // 2], S, on_vector=True)
 
-        gated = {}
-
-        def apply_gate(lo, hi, tag):
-            made = tile([P, (hi - lo) * C], F32, f"gated{lo}", tag)
-            nc.vector.tensor_tensor(made[:], acts[:, lo * C : hi * C], gate_of(lo, hi), MULT)
-            for e in range(lo, hi):
-                gated[e] = made[:, (e - lo) * C : (e - lo + 1) * C]
-
-        def scatter_gated(e):
-            nc.scalar.activation(windows[1][:].indirect(places(e, e + 1)), gated[e], COPY)
-
-        gather_row(0, 2, 0, S // 2)
-        gather_row(0, 2, S // 2, S)
-        round_pair(0, 0)
-        round_pair(0, 1)
-        gather_pair(0)
-        for i in range(3):
-            gather_row(0, 3, i * PIECE, (i + 1) * PIECE)
-        woven0 = [tile([P, 2 * PIECE], U32, f"woven0_{i}") for i in range(2)]
+        for r in range(PACK):
+            gather_shared(r)
+        woven0 = [weave(0, lo, lo + PIECE) for lo in range(0, S, PIECE)]
         for i in range(2):
-            weave(0, i * PIECE, (i + 1) * PIECE, woven0[i][:])
-        for i in range(2):
-            quantize(0, i * PIECE, (i + 1) * PIECE, woven0[i][:])
-        round_pair(1, 0)
-        woven0.append(tile([P, 2 * PIECE], U32, "woven0_2", "raw1_0"))
-        weave(0, 2 * PIECE, S, woven0[2][:], on_scalar=True)
-        round_pair(1, 1)
-        gather_pair(1)
-        quantize(0, 2 * PIECE, S, woven0[2][:])
-
-        gather_row(1, 2, 0, PIECE)
-        gather_row(1, 2, PIECE, 2 * PIECE)
-        for e in range(EARLY):
-            product(0, e)
-        woven1 = {1: picked[1][:, S + 2 * PIECE :]}
-
-        def weave1(e, tag=None):
-            if e not in woven1:
-                woven1[e] = tile([P, 2 * C], U32, f"woven1_{e}", tag)[:]
-            weave(1, e * C, (e + 1) * C, woven1[e])
-
-        def finish(e):
-            quantize(1, e * C, (e + 1) * C, woven1[e])
-
-        def multiply(e):
-            product(1, e)
-            if e >= EARLY:
-                product(0, e)
-
-        for e in range(4):
-            gather_row(1, 3, e * C, (e + 1) * C)
-        weave1(0)
-        weave1(1)
-        finish(0)
-        multiply(0)
-        finish(1)
-        multiply(1)
+            gather_shared(PACK + i)
+            quantize(0, i * PIECE, (i + 1) * PIECE, woven0[i])
+        gather_row(1, 2, C, 2 * PIECE)
         gather_row(1, 2, 2 * PIECE, S)
-        gather_row(1, 3, 4 * C, 5 * C)
-        gather_row(1, 3, 5 * C, 6 * C)
-        weave1(2)
-        weave1(3)
-        finish(2)
-        multiply(2)
-        finish(3)
-        multiply(3)
-        relu(0, on_vector=True)
-        relu(1)
-        relu(2)
-        relu(3)
-        weave1(4, "codes1_0")
-        apply_gate(0, 1, None)
-        scatter_gated(0)
-        weave1(5, f"codes1_{C}")
-        finish(4)
-        multiply(4)
-        finish(5)
-        multiply(5)
-        relu(4)
-        relu(5)
-        scatter_gating(1, 2)
-        apply_gate(2, 4, f"codes1_{5 * C}")
-        scatter_gated(2)
-        scatter_gated(3)
-        scatter_gating(4, 6)
+        gather_row(1, 2, 0, C, on_vector=True)
+        quantize(0, 2 * PIECE, S, woven0[2])
+        for e in range(E):
+            gather_row(1, 3, e * C, (e + 1) * C, on_vector=e == 0)
+        for e in range(E):
+            product(0, e)
+        woven1 = [weave(1, 0, C)]
+        for e in range(E):
+            if e + 1 < E:
+                woven1.append(weave(1, (e + 1) * C, (e + 2) * C))
+            quantize(1, e * C, (e + 1) * C, woven1[e])
+            product(1, e)
+        for e in range(E):
+            relu(e)
+        gated = tile([P, SHARED], F32, "gated")
+        for lo in range(0, SHARED, SCATTER):
+            nc.vector.tensor_tensor(gated[:, lo : lo + SCATTER], acts[:, lo : lo + SCATTER], gates[0][:, lo : lo + SCATTER], MULT)
+        for lo in range(0, SHARED, SCATTER):
+            nc.scalar.activation(windows[1][:].indirect(places(lo, lo + SCATTER)), gated[:, lo : lo + SCATTER], COPY)
+        nc.vector.tensor_tensor(windows[0][:].indirect(places(SHARED, S)), acts[:, SHARED:], gates[1][:], MULT)
         for i, lo in enumerate(range(0, T, STORE)):
             total = tile([P, STORE], F32, f"total{i}")
             nc.vector.tensor_tensor(total[:], windows[0][:, lo : lo + STORE], windows[1][:, lo : lo + STORE], ADD)

@@ -39,7 +39,7 @@ def tile_moe_two_lin_relu_kernel(
         psum = ctx.enter_context(tc.psum_pool(name="psum", bufs=E))
 
         def tile(shape, dtype, name, tag=None):
-            return keep.tile(shape, dtype, name=name, tag=tag or name, align_bytes=64)
+            return keep.tile(shape, dtype, name=name, tag=tag or name, align_bytes=256)
 
         offs_sb = keep.tile([P, S // 16], U16, name="offs_sb")
         dst_sb = keep.tile([P, S // 16], U16, name="dst_sb")

@@ -24,7 +24,7 @@ P = 128
 PACK = 4
 K_PASS = P * PACK
 PIECE = 2 * C
-VECTOR_FROM = (768, 768, 928)
+VECTOR_FROM = (768, 928, 832)
 SHARED = 3 * C
 SCATTER = SHARED // 2
 STORE = 512
@@ -80,24 +80,16 @@ def tile_moe_two_lin_relu_kernel(
 
         load_row(0, 0)
         nc.sync.dma_start(offs_sb[:], offs)
+        for a, j in ((0, 1), (0, 2), (0, 3), (1, 2), (1, 0), (1, 1), (1, 3)):
+            load_row(a, j)
+        for a in range(2):
+            load_weights(a)
+            for q in range(4):
+                load_scales(a, q)
         nc.sync.dma_start(out=bias[:], in_=b)
-        load_row(0, 1)
-        load_row(0, 2)
-        load_scales(0, 0)
-        load_scales(0, 1)
-        load_row(0, 3)
-        load_scales(0, 2)
-        load_scales(0, 3)
-        load_row(1, 0)
-        nc.sync.dma_start(dst_sb[:], dst)
-        for j in range(1, PACK):
-            load_row(1, j)
-        load_weights(0)
-        load_weights(1)
-        for q in range(4):
-            load_scales(1, q)
         gates = [tile([P, hi - lo], F32, f"gate{lo}") for lo, hi in ((0, SHARED), (SHARED, S))]
         nc.sync.dma_start(out=gates[0][:], in_=gate[:, :SHARED])
+        nc.sync.dma_start(dst_sb[:], dst)
         nc.sync.dma_start(out=gates[1][:], in_=gate[:, SHARED:])
 
         both = tile([P, 4 * S], U32, "picked")
@@ -158,26 +150,31 @@ def tile_moe_two_lin_relu_kernel(
             gather_row(a, j, 0, VECTOR_FROM[r // 2])
             gather_row(a, j, VECTOR_FROM[r // 2], S, on_vector=True)
 
-        for r in range(PACK):
+        for r in range(PACK - 1):
             gather_shared(r)
-        woven0 = [weave(0, lo, lo + PIECE) for lo in range(0, S, PIECE)]
-        for i in range(2):
-            gather_shared(PACK + i)
-            quantize(0, i * PIECE, (i + 1) * PIECE, woven0[i])
+        gather_row(0, 3, 0, PIECE)
+        gather_row(0, 3, PIECE, VECTOR_FROM[1])
+        gather_row(0, 3, VECTOR_FROM[1], S, on_vector=True)
+        woven0 = {lo: weave(0, lo, lo + PIECE) for lo in (2 * PIECE, 0, PIECE)}
         gather_row(1, 2, C, 2 * PIECE)
         gather_row(1, 2, 2 * PIECE, S)
         gather_row(1, 2, 0, C, on_vector=True)
-        quantize(0, 2 * PIECE, S, woven0[2])
+        for lo in woven0:
+            quantize(0, lo, lo + PIECE, woven0[lo])
+        gather_shared(PACK)
+        gather_shared(PACK + 1)
         for e in range(E):
             gather_row(1, 3, e * C, (e + 1) * C, on_vector=e == 0)
         for e in range(E):
             product(0, e)
-        woven1 = [weave(1, 0, C)]
-        for e in range(E):
-            if e + 1 < E:
-                woven1.append(weave(1, (e + 1) * C, (e + 2) * C))
-            quantize(1, e * C, (e + 1) * C, woven1[e])
-            product(1, e)
+        cuts = (0, 2, 3, 4, 5, 6)
+        woven1 = [weave(1, 0, cuts[1] * C)]
+        for i, (lo, hi) in enumerate(zip(cuts, cuts[1:])):
+            if hi < E:
+                woven1.append(weave(1, hi * C, cuts[i + 2] * C))
+            quantize(1, lo * C, hi * C, woven1[i])
+            for e in range(lo, hi):
+                product(1, e)
         for e in range(E):
             relu(e)
         gated = tile([P, SHARED], F32, "gated")

@@ -24,7 +24,8 @@ P = 128
 PACK = 4
 K_PASS = P * PACK
 PIECE = 2 * C
-VECTOR_FROM = (768, 928, 832)
+VECTOR_FROM = (768, 928, 800)
+AHEAD = 3
 SHARED = 3 * C
 SCATTER = SHARED // 2
 STORE = 512
@@ -82,10 +83,13 @@ def tile_moe_two_lin_relu_kernel(
         nc.sync.dma_start(offs_sb[:], offs)
         for a, j in ((0, 1), (0, 2), (0, 3), (1, 2), (1, 0), (1, 1), (1, 3)):
             load_row(a, j)
+        scale_loads = [(a, q) for a in range(2) for q in range(4)]
+        for a, q in scale_loads[:AHEAD]:
+            load_scales(a, q)
         for a in range(2):
             load_weights(a)
-            for q in range(4):
-                load_scales(a, q)
+        for a, q in scale_loads[AHEAD:]:
+            load_scales(a, q)
         nc.sync.dma_start(out=bias[:], in_=b)
         gates = [tile([P, hi - lo], F32, f"gate{lo}") for lo, hi in ((0, SHARED), (SHARED, S))]
         nc.sync.dma_start(out=gates[0][:], in_=gate[:, :SHARED])
@@ -108,18 +112,18 @@ def tile_moe_two_lin_relu_kernel(
             else:
                 nc.scalar.activation(to, rows[a, j][:].indirect(listed(lo, hi)), COPY)
 
+        woven = [tile([P, 2 * S], U32, f"woven{a}") for a in range(2)]
+
         def weave(a, lo, hi):
-            woven = tile([P, 2 * (hi - lo)], U32, f"woven{a}_{lo}")
-            to = woven[:].rearrange("p (c i u) -> p c u i", i=2, u=2)
+            to = woven[a][:, 2 * lo : 2 * hi].rearrange("p (c i u) -> p c u i", i=2, u=2)
             source = picked[a].rearrange("p (u s) -> p u s", u=2)[:, :, lo:hi].rearrange("p u (c i) -> p c u i", i=2)
             nc.vector.tensor_copy(out=to, in_=source)
-            return woven[:]
 
         codes = {}
 
-        def quantize(a, lo, hi, woven):
+        def quantize(a, lo, hi):
             made = tile([P, hi - lo], U32, f"codes{a}_{lo}")
-            nc.vector.quantize_mx(out=made[:].bitcast(E4M3X4), scales=planes[a][:, lo:hi], in_=woven.bitcast(BF16))
+            nc.vector.quantize_mx(out=made[:].bitcast(E4M3X4), scales=planes[a][:, lo:hi], in_=woven[a][:, 2 * lo : 2 * hi].bitcast(BF16))
             for e in range(lo // C, hi // C):
                 codes[a, e] = made[:, e * C - lo : (e + 1) * C - lo]
 
@@ -155,24 +159,26 @@ def tile_moe_two_lin_relu_kernel(
         gather_row(0, 3, 0, PIECE)
         gather_row(0, 3, PIECE, VECTOR_FROM[1])
         gather_row(0, 3, VECTOR_FROM[1], S, on_vector=True)
-        woven0 = {lo: weave(0, lo, lo + PIECE) for lo in (2 * PIECE, 0, PIECE)}
-        gather_row(1, 2, C, 2 * PIECE)
-        gather_row(1, 2, 2 * PIECE, S)
-        gather_row(1, 2, 0, C, on_vector=True)
-        for lo in woven0:
-            quantize(0, lo, lo + PIECE, woven0[lo])
+        for lo in (2 * PIECE, 0, PIECE):
+            weave(0, lo, lo + PIECE)
+        gather_row(1, 2, 0, C)
+        gather_row(1, 2, 2 * C, S)
+        gather_row(1, 2, C, 2 * C, on_vector=True)
+        quantize(0, 2 * PIECE, S)
+        quantize(0, 0, 2 * PIECE)
         gather_shared(PACK)
         gather_shared(PACK + 1)
         for e in range(E):
-            gather_row(1, 3, e * C, (e + 1) * C, on_vector=e == 0)
+            gather_row(1, 3, e * C, (e + 1) * C, on_vector=e == 1)
         for e in range(E):
             product(0, e)
+        weave(1, 0, C)
+        weave(1, C, 2 * C)
         cuts = (0, 2, 3, 4, 5, 6)
-        woven1 = [weave(1, 0, cuts[1] * C)]
-        for i, (lo, hi) in enumerate(zip(cuts, cuts[1:])):
+        for lo, hi in zip(cuts, cuts[1:]):
             if hi < E:
-                woven1.append(weave(1, hi * C, cuts[i + 2] * C))
-            quantize(1, lo * C, hi * C, woven1[i])
+                weave(1, hi * C, (hi + 1) * C)
+            quantize(1, lo * C, hi * C)
             for e in range(lo, hi):
                 product(1, e)
         for e in range(E):

@@ -28,7 +28,7 @@ VECTOR_FROM = (768, 928, 800)
 AHEAD = 3
 SHARED = 3 * C
 SCATTER = SHARED // 2
-STORE = 512
+STORE_CUTS = (0, 384, 864, 1408, T)
 
 
 def tile_moe_two_lin_relu_kernel(
@@ -189,7 +189,7 @@ def tile_moe_two_lin_relu_kernel(
         for lo in range(0, SHARED, SCATTER):
             nc.scalar.activation(windows[1][:].indirect(places(lo, lo + SCATTER)), gated[:, lo : lo + SCATTER], COPY)
         nc.vector.tensor_tensor(windows[0][:].indirect(places(SHARED, S)), acts[:, SHARED:], gates[1][:], MULT)
-        for i, lo in enumerate(range(0, T, STORE)):
-            total = tile([P, STORE], F32, f"total{i}")
-            nc.vector.tensor_tensor(total[:], windows[0][:, lo : lo + STORE], windows[1][:, lo : lo + STORE], ADD)
-            (nc.sync, nc.scalar)[i % 2].dma_start(out=out[:, lo : lo + STORE], in_=total[:])
+        for i, (lo, hi) in enumerate(zip(STORE_CUTS, STORE_CUTS[1:])):
+            total = tile([P, hi - lo], F32, f"total{i}")
+            nc.vector.tensor_tensor(total[:], windows[0][:, lo:hi], windows[1][:, lo:hi], ADD)
+            (nc.sync, nc.scalar)[i % 2].dma_start(out=out[:, lo:hi], in_=total[:])

from contextlib import ExitStack

import concourse.mybir as mybir

K, T, E, C, N = 1024, 2048, 6, 256, 128
S = E * C

F32 = mybir.dt.float32
BF16 = mybir.dt.bfloat16
I32 = mybir.dt.int32
U32 = mybir.dt.uint32
U16 = mybir.dt.uint16
U8 = mybir.dt.uint8
E4M3X4 = mybir.dt.float8_e4m3fn_x4
E2M1X4 = mybir.dt.float4_e2m1fn_x4
COPY = mybir.ActivationFunctionType.Copy
RELU = mybir.ActivationFunctionType.Relu
MULT = mybir.AluOpType.mult
ADD = mybir.AluOpType.add

FLOPS = 2 * K * N * S

P = 128
PACK = 4
K_PASS = P * PACK
PIECE = 2 * C
VECTOR_FROM = (768, 928, 800)
AHEAD = 3
SHARED = 3 * C
SCATTER = SHARED // 2
STORE_CUTS = (0, 384, 864, 1408, T)


def tile_moe_two_lin_relu_kernel(
    tc, xT, w8_words, w8_scales, w4_words, w4_scales, b, gate, offs, dst, out
):
    nc = tc.nc
    with ExitStack() as ctx:
        keep = ctx.enter_context(tc.tile_pool(name="keep", bufs=1))
        psum = ctx.enter_context(tc.psum_pool(name="psum", bufs=E))

        def tile(shape, dtype, name, tag=None):
            return keep.tile(shape, dtype, name=name, tag=tag or name, align_bytes=256)

        offs_sb = keep.tile([P, S // 16], U16, name="offs_sb")
        dst_sb = keep.tile([P, S // 16], U16, name="dst_sb")
        w_planes = [tile([P, E, N], U8, f"w_planes{a}") for a in range(2)]
        windows = [tile([P, T], F32, f"window{i}") for i in range(2)]
        for a in range(2):
            nc.gpsimd.memset(w_planes[a][:].bitcast(I32), 0)

        nc.vector.memset(windows[0][:, : T // 2], 0.0)
        nc.scalar.activation(windows[1][:, : T // 2], windows[0][:, : T // 2], COPY)
        for window in windows:
            nc.vector.memset(window[:, T // 2 :], 0.0)

        by_row = [xT[a * K_PASS : (a + 1) * K_PASS, :].rearrange("(p j) w -> p j w", j=PACK) for a in range(2)]
        rows = {}

        def load_row(a, j):
            rows[a, j] = tile([P, T], F32, f"row{a}_{j}")
            nc.sync.dma_start(out=rows[a, j][:], in_=by_row[a][:, j, :])

        def load_scales(a, q):
            scales = (w8_scales, w4_scales)[a]
            nc.sync.dma_start(
                out=w_planes[a][32 * q : 32 * q + 4].bitcast(I32),
                in_=scales[:, :, 4 * q : 4 * q + 4, :].rearrange("e a q n -> q (e a) n").bitcast(I32),
            )

        w_rows = (w8_words.rearrange("e a p n r -> p (e a) (n r)"), w4_words.rearrange("e a p n -> p (e a) n"))
        w_sb = {}

        def load_weights(a):
            part = tile([P, E, w_rows[a].shape[2]], U8, f"w{a}")
            nc.sync.dma_start(out=part[:].bitcast(I32), in_=w_rows[a].bitcast(I32))
            for e in range(E):
                w_sb[a, e] = part[:, e, :]

        bias = tile([P, E], F32, "bias")

        load_row(0, 0)
        nc.sync.dma_start(offs_sb[:], offs)
        for a, j in ((0, 1), (0, 2), (0, 3), (1, 2), (1, 0), (1, 1), (1, 3)):
            load_row(a, j)
        scale_loads = [(a, q) for a in range(2) for q in range(4)]
        for a, q in scale_loads[:AHEAD]:
            load_scales(a, q)
        for a in range(2):
            load_weights(a)
        for a, q in scale_loads[AHEAD:]:
            load_scales(a, q)
        nc.sync.dma_start(out=bias[:], in_=b)
        gates = [tile([P, hi - lo], F32, f"gate{lo}") for lo, hi in ((0, SHARED), (SHARED, S))]
        nc.sync.dma_start(out=gates[0][:], in_=gate[:, :SHARED])
        nc.sync.dma_start(dst_sb[:], dst)
        nc.sync.dma_start(out=gates[1][:], in_=gate[:, SHARED:])

        both = tile([P, 4 * S], U32, "picked")
        picked = [both[:, 2 * S * a : 2 * S * (a + 1)] for a in range(2)]
        planes = [tile([P, S], U8, f"planes{a}") for a in range(2)]
        acts = tile([P, S], F32, "acts")

        def listed(lo, hi):
            return offs_sb[:, lo // 16 : hi // 16]

        def gather_row(a, j, lo, hi, on_vector=False):
            half = S * (j // 2)
            to = picked[a][:, half + lo : half + hi].bitcast(BF16).rearrange("p (s h) -> p s h", h=2)[:, :, j % 2]
            if on_vector:
                nc.vector.tensor_copy(to, rows[a, j][:].indirect(listed(lo, hi)))
            else:
                nc.scalar.activation(to, rows[a, j][:].indirect(listed(lo, hi)), COPY)

        woven = [tile([P, 2 * S], U32, f"woven{a}") for a in range(2)]

        def weave(a, lo, hi):
            to = woven[a][:, 2 * lo : 2 * hi].rearrange("p (c i u) -> p c u i", i=2, u=2)
            source = picked[a].rearrange("p (u s) -> p u s", u=2)[:, :, lo:hi].rearrange("p u (c i) -> p c u i", i=2)
            nc.vector.tensor_copy(out=to, in_=source)

        codes = {}

        def quantize(a, lo, hi):
            made = tile([P, hi - lo], U32, f"codes{a}_{lo}")
            nc.vector.quantize_mx(out=made[:].bitcast(E4M3X4), scales=planes[a][:, lo:hi], in_=woven[a][:, 2 * lo : 2 * hi].bitcast(BF16))
            for e in range(lo // C, hi // C):
                codes[a, e] = made[:, e * C - lo : (e + 1) * C - lo]

        accs = {}

        def product(a, e):
            first = e not in accs
            if first:
                accs[e] = psum.tile([P, C], F32, name="acc")
            nc.tensor.matmul_mx(
                out=accs[e][:],
                lhsT=w_sb[a, e].bitcast((E4M3X4, E2M1X4)[a]),
                lhsT_scale=w_planes[a][:, e, :],
                rhs=codes[a, e].bitcast(E4M3X4),
                rhs_scale=planes[a][:, e * C : (e + 1) * C],
                start=first,
                stop=not first,
            )

        def relu(e):
            nc.scalar.activation(acts[:, e * C : (e + 1) * C], accs[e][:], RELU, bias=bias[:, e : e + 1])

        def places(lo, hi):
            return dst_sb[:, lo // 16 : hi // 16]

        def gather_shared(r):
            a, j = divmod(r, PACK)
            gather_row(a, j, 0, VECTOR_FROM[r // 2])
            gather_row(a, j, VECTOR_FROM[r // 2], S, on_vector=True)

        for r in range(PACK - 1):
            gather_shared(r)
        gather_row(0, 3, 0, PIECE)
        gather_row(0, 3, PIECE, VECTOR_FROM[1])
        gather_row(0, 3, VECTOR_FROM[1], S, on_vector=True)
        for lo in (2 * PIECE, 0, PIECE):
            weave(0, lo, lo + PIECE)
        gather_row(1, 2, 0, C)
        gather_row(1, 2, 2 * C, S)
        gather_row(1, 2, C, 2 * C, on_vector=True)
        quantize(0, 2 * PIECE, S)
        quantize(0, 0, 2 * PIECE)
        gather_shared(PACK)
        gather_shared(PACK + 1)
        for e in range(E):
            gather_row(1, 3, e * C, (e + 1) * C, on_vector=e == 1)
        for e in range(E):
            product(0, e)
        weave(1, 0, C)
        weave(1, C, 2 * C)
        cuts = (0, 2, 3, 4, 5, 6)
        for lo, hi in zip(cuts, cuts[1:]):
            if hi < E:
                weave(1, hi * C, (hi + 1) * C)
            quantize(1, lo * C, hi * C)
            for e in range(lo, hi):
                product(1, e)
        for e in range(E):
            relu(e)
        gated = tile([P, SHARED], F32, "gated")
        for lo in range(0, SHARED, SCATTER):
            nc.vector.tensor_tensor(gated[:, lo : lo + SCATTER], acts[:, lo : lo + SCATTER], gates[0][:, lo : lo + SCATTER], MULT)
        for lo in range(0, SHARED, SCATTER):
            nc.scalar.activation(windows[1][:].indirect(places(lo, lo + SCATTER)), gated[:, lo : lo + SCATTER], COPY)
        nc.vector.tensor_tensor(windows[0][:].indirect(places(SHARED, S)), acts[:, SHARED:], gates[1][:], MULT)
        for i, (lo, hi) in enumerate(zip(STORE_CUTS, STORE_CUTS[1:])):
            total = tile([P, hi - lo], F32, f"total{i}")
            nc.vector.tensor_tensor(total[:], windows[0][:, lo:hi], windows[1][:, lo:hi], ADD)
            (nc.sync, nc.scalar)[i % 2].dma_start(out=out[:, lo:hi], in_=total[:])
